import numpy as np, ml_dtypes
CORES = [35,38,43,46]
N = 4
import mx_ref
BF = ml_dtypes.bfloat16
def gentries(a):
    return np.ascontiguousarray(a.reshape(8, 16, -1).transpose(0, 2, 1)).reshape(8, -1)
def gtable(e):
    e = np.asarray(e); return np.ascontiguousarray(e.reshape(8, -1, 16).transpose(0, 2, 1)).reshape(128, -1).astype(np.int32)
def gcols(t, e):
    v = np.concatenate([t.reshape(8, 16, -1, 4), np.zeros((8, 16, 1, 4), BF)], axis=2)
    return np.ascontiguousarray(np.stack([v[g][:, e[g]] for g in range(8)])).reshape(128, -1)
def tile(rs):
    return np.stack(rs, axis=2).reshape(128, -1).astype(BF)
def pick(q, e):
    c = np.concatenate([q[0].reshape(128, -1, 4), np.zeros((128, 1, 4), np.uint8)], axis=1); s = np.concatenate([q[1], np.ones((16, 1), np.uint8)], axis=1)
    return (np.ascontiguousarray(c[:, e].reshape(128, -1)), np.ascontiguousarray(s[:, e]))
def join(*qs):
    return (np.concatenate([q[0] for q in qs], axis=1), np.concatenate([q[1] for q in qs], axis=1))
def put(q, e, v):
    c, s = q[0].reshape(128, -1, 4).copy(), q[1].copy(); c[:, e] = v[0].reshape(128, -1, 4); s[:, e] = v[1]
    return (c.reshape(128, -1), s)
def pk(c, s):
    return (np.ascontiguousarray(c), mx_ref.live(s))
def emit(q):
    return q[0], q[1]
def packed(v, rng):
    q = [mx_ref.quantize(np.ascontiguousarray(v[r])) for r in range(N)]
    return np.stack([a for a, b in q]), np.stack([mx_ref.plane(b, rng) for a, b in q])
def values_of_codes():
    e, c = np.zeros((128, 128, 4), np.float32), np.zeros((128, 2, 4), np.uint8)
    e[np.arange(128), np.arange(128), 0] = 1
    c[:127, :, 0] = np.arange(256).reshape(2, 128).T[:127]
    return mx_ref.matmul(mx_ref.quantize(e.reshape(128, 512).astype(BF)), (c.reshape(128, 8), np.full((16, 2), 127, np.uint8))).T.reshape(-1).astype(np.float64)
CODE_VALUE, SCALE_VALUE = values_of_codes(), 2.0 ** (np.arange(256) - 127.0)
def decode(q):
    return (CODE_VALUE[q[0]].reshape(16, 8, -1, 4) * SCALE_VALUE[q[1]][:, None, :, None] + 0.0).reshape(128, -1).astype(np.float32)
def f(rng, *shape):
    return mx_ref.flush((rng.standard_normal(shape, dtype=np.float32) * np.exp2(rng.integers(-2, 3, shape[:-1] + (1,)))).astype(BF))
def wide(rng, *shape, cols=0):
    v = rng.standard_normal(shape, dtype=np.float32) * np.exp2(rng.integers(-12, 13, shape)).astype(np.float32)
    if cols: v *= np.repeat(np.exp2(rng.integers(-cols, cols + 1, shape[:-2] + (1, shape[-1] // 4))) * (rng.random(shape[:-2] + (1, shape[-1] // 4)) > 0.0625), 4, axis=-1).astype(np.float32)
    return mx_ref.flush(v.astype(BF))
C, H, R = 448, 192, 2
def follow(copies, far):
    e = np.tile(np.arange(H + C), (8, 1))
    e[:, H:] -= np.where(copies, far, 0)
    for i in range(C.bit_length()): e = np.take_along_axis(e, e, axis=1)
    return e[:, H:]
def alike(a):
    return np.stack([a] * N)
def trim(v):
    v = v.astype(np.float32)
    v[np.abs(v) < np.float32(2.0 ** -16)] = 0
    return v.astype(BF)
def weights(rng, shut=np.zeros(128, bool)):
    w = trim(f(rng, 128, 2048)).reshape(128, 4, 128, 4)
    w[shut] = 0
    w[:, :, shut] = 0
    c, p = packed(alike(w.reshape(128, 2048)), rng)
    return {"wc": c, "ws": p}
def numbers_of(rng):
    return {"x": trim(f(rng, N, 128, 4 * C)), "u": alike(np.array(f(rng, 128, 512))), "v": np.array(f(rng, N, 128, 512)), "dist": alike(gtable(rng.integers(1, H + 1, (8, C))))}
def first():
    return np.arange(128) % 16 < 8
def heads(d, s, a, b):
    x = d["x"].reshape(N, 8, 16, C, 4)
    x[:, :, :8] = (s * a).astype(np.float32).astype(BF)[:, :, None, :, None]
    u = d["u"].reshape(N, 8, 16, 8, 16, 4)
    u[:, :, :, :, 0] = 0
    for g in range(8): u[:, g, :8, g, 0] = b[g]
    return {**d, "x": x.reshape(N, 128, 4 * C), "u": u.reshape(N, 128, 512)}
def setup_inputs(rng):
    return {**numbers_of(rng), **weights(rng)}
def setup_inputs_deep(rng):
    d = numbers_of(rng)
    k = rng.permutation(8)
    far = rng.integers(1, H + 1, (8, C))
    far[k[:4]] = 1
    far[k[4:6]] = H
    s = rng.permuted(np.tile(np.arange(C) % 2 * 2.0 - 1.0, (N, 8, 1)), axis=2)
    for i in (0, 1, 2, 4, 6): s[:, k[i]] = -1
    s[:, k[1], 0] = 1
    for r in range(N): s[r, k[2], rng.permutation(C)[:3]] = 1
    s[:, k[3]] = (rng.permutation(N) % 2 * 2.0 - 1.0)[:, None]
    d["dist"] = alike(gtable(far))
    return {**heads(d, s, 1.0, [1.0] * 8), **weights(rng, first())}
def setup_inputs_near(rng):
    d = numbers_of(rng)
    s = rng.permuted(np.tile(np.arange(C) % 3 - 1.0, (N, 8, 1)), axis=2)
    k = rng.permutation(8)
    h = int(rng.integers(8))
    d = heads(d, s, np.where(k < 6, 2.0 ** -23, 2.0 ** -30)[:, None], [1.0 if k[g] < 4 else 2.0 ** -25 if k[g] < 6 else 2.0 ** -30 for g in range(8)])
    x = d["x"].reshape(N, 8, 16, C, 4)
    x[:, :, 1:8] = 0
    x[:, :, 0, :, 1:] = 0
    x[:, h, 8:] = 0
    x[:, h, 8, :, 0] = 1
    x[:, h, 9, :, 0] = -1
    u = d["u"].reshape(N, 8, 16, 8, 16, 4)
    for g in range(8):
        if k[g] < 4: u[:, h, 8:10, g, 0, 0] = 1
    shut = first()
    shut[16 * h:16 * h + 16] = True
    return {**d, "x": x.reshape(N, 128, 4 * C), "u": u.reshape(N, 128, 512), **weights(rng, shut)}
def setup_inputs_sums(rng):
    d = numbers_of(rng)
    g = 4 + 2 * int(rng.integers(2))
    blk = np.array([4, 5, 6, 7, 2 * g, 2 * g + 1, 2 * g + 2, 2 * g + 3])
    rest = rng.permutation(np.setdiff1d(np.arange(16), blk))
    x = np.zeros((N, 16, 8, C, 4), np.float32)
    w = np.zeros((128, 4, 128, 4), np.float32)
    u = d["u"].reshape(N, 128, 128, 4)
    u[:, :, ::16] = 0
    r, j = np.arange(N)[:, None], np.arange(C)
    o = np.argsort(rng.random((N, C, 8)), axis=2)
    for h in range(8):
        p, b = h // 4, h % 4
        i = np.take_along_axis(o[:, :, :4], np.argsort(rng.random((N, C, 4)), axis=2), axis=2)
        s = np.take_along_axis(o[:, :, 4:], rng.integers(0, 4, (N, C, 1)), axis=2)
        x[r, blk[i[:, :, 0]], p, j, b] = 1
        x[r, blk[i[:, :, 1]], p, j, b] = -1
        x[r, blk[s[:, :, 0]], p, j, b] = rng.choice([-1.0, 1.0], (N, C)) * 2.0 ** -26
        x[:, rest[h], 0, :, 0] = rng.integers(1, 9, (N, C)) * rng.choice([-1.0, 1.0], (N, C)) * 2.0 ** -26
        u[:, 8 * blk + p, 16 * h, b] = 1
        w[8 * blk + p, 0, 8 * rest[h], b] = 64
    c, q = packed(alike(w.reshape(128, 2048).astype(BF)), rng)
    return {**d, "x": x.reshape(N, 128, 4 * C).astype(BF), "u": u.reshape(N, 128, 512), "wc": c, "ws": q}
def setup_inputs_huge(rng):
    d = numbers_of(rng)
    s = rng.permuted(np.tile(np.arange(C) % 2 * 2.0 - 1.0, (N, 8, 1)), axis=2)
    k = rng.permutation(8)
    s[:, k[0]] = -1
    s[:, k[1]] = 1
    return {**heads(d, s, 2.0 ** 30, [2.0 ** 30] * 8), **weights(rng, first())}
def setup_inputs_spread(rng):
    d = setup_inputs(rng)
    d["x"] = trim(wide(rng, N, 128, 4 * C, cols=6))
    return d
def check_inputs(d):
    b = []
    for k in ("x", "u", "v"):
        a = np.abs(d[k].astype(np.float32))
        if not (np.isfinite(a).all() and ((a == 0) | (a >= 2.0 ** -30) & (a <= 2.0 ** 30)).all()): b.append("a value of " + k)
    for k in ("u", "wc", "dist"):
        if (d[k] != d[k][:1]).any(): b.append(k + " differs between ranks")
    s = [mx_ref.live(p) for p in d["ws"]]
    if any((p != s[0]).any() for p in s): b.append("ws differs between ranks")
    if ((d["wc"] == 127) | (d["wc"] == 255)).any(): b.append("a code of wc")
    if (d["dist"] < 1).any() or (d["dist"] > H).any(): b.append("a number of dist")
    return b
def reference(x, u, v, dist, wc, ws):
    w, qu, far = pk(wc[0], ws[0]), mx_ref.quantize(u[0]), gentries(dist[0])
    now = [x[r] for r in range(N)]
    for t in range(R):
        q = [mx_ref.quantize(now[r]) for r in range(N)]
        full = [decode(q[r]) for r in range(N)]
        roots = []
        for r in range(N):
            e = follow(mx_ref.matmul(qu, q[r])[::16] < 0, far)
            halo = full[r - 1][:, 4 * (C - H):] if r > 0 else np.zeros((128, 4 * H), np.float32)
            z = mx_ref.quantize(gcols(np.concatenate([halo, full[r]], axis=1).astype(BF), e))
            now[r] = tile([full[r][:, b::4] + mx_ref.matmul(pick(w, np.arange(128 * b, 128 * b + 128)), z) * np.float32(0.015625) for b in range(4)])
            roots.append(e - H)
    y, ol = np.zeros((N, 128, C), np.float32), np.zeros((N, 8, C), np.float32)
    oc, osc = np.zeros((N, 128, 4 * C), np.uint8), np.zeros((N, 16, C), np.uint8)
    for r in range(N):
        last = mx_ref.quantize(now[r])
        y[r] = mx_ref.matmul(mx_ref.quantize(v[r]), last)
        ol[r] = roots[r]
        oc[r], osc[r] = emit(last)
    return {"y": y, "ol": ol, "oc": oc, "osc": osc}

@@ -1,0 +1,396 @@
+from concourse.mybir import dt, AluOpType, ActivationFunctionType
+
+C, H, ROUNDS = 448, 192, 2
+M = C // 16
+B0 = 4 * H
+WW = B0 + C
+A1, A2, A3 = [(0, C)], [(0, C - H), (C - H, C)], [(0, 160), (160, 320), (320, C)]
+CFG = {"K": 5, "LCH": A2, "VCH": [A2, A2], "TCH": [A2, A2, A3], "FCH": [A1, A1]}
+ORDER = """
+g64V cs4V cs1V lddY t16G ipG i16G pmiV pmV selG ldx1S d0V it0V lpV pm1V cor0V he1V jwV uoV d1V hw1V d2V it1V qe2V a0V
+hw0S lduY lnV a1V a2V ddS corrV l0V qe0V wg00S wg10S wg01V ldx0Y qt01V quV par0S cs10V ct10V wg11S cs11V puV pusS ct11V
+qt00V mp01T wg20S cs20V wg21S sg01S mp00T cs21V ct20V snd0G ct21V wg30V mf000T sg00S fl00V he0S fl01V fx0V wg31S cs30V
+qe1V cs31V ct30V sh000S vs000V mf002T sh001S arr0R vs001V mf001T wg40S sh010S sh011S cs40V fe002S mh02T ct31V ldsY mh01T
+vs010V vs011V sh021S sh020V mh00T ct40V vs020V wg41S vs021V sh030S qe3V wg50S vs030V sh031S cs41V mf003T cs50V vs031V
+ct50V sh040S fe001S mh03T ct41V wg51S vs040V sh041V bl01V he01S pl0G bl02V fe000S vs041V he00S he02S ldwY bl03V cs51V
+fe003S bl04V ct51V he03S bl05V bl06V bl07V bl08V csr00V bl09V ctr00V zg000S ldvY bl010V zg001S bl011V bl012V bl013V
+zg003V csr01V ctr01V me000T zg002S me001T qz00V zg010V me002T me011T me003T me012T me010T zg013S zg012S mw001T zg011V
+mw000T mw003T mw002T qz01V me013T te001S mw013T te000S te003S mw012T pl1G mw011T mw010T te013S te012S te002V qt10V mp10T
+te011V te010S sg10S qt11V mp11T snd1G fl10V mf101T fx1V mf103T sh100V sg11S fl11V vs100V sh101S mf100T vs101V sh110S
+arr1R mf102T vs110V sh111S sh120S vs111V mh10T sh121V vs120V mh13T vs121V fe102S sh130S sh131S fe100S qvV fe101S vs130V
+vs131V mh11T he13S sh140V he11S mh12T sh141V vs140V fe103S bl11V bl12V bl13V bl14V he10S bl15V he12S csr10V bl16V ctr10V
+zg103S zg100S vs141V bl17V zg102S bl18V bl19V csr11V me101T zg101S me100T bl110V ctr11V bl111V bl112V zg110S me113T
+me102T me103T zg111S qz10V mw103T mw101T zg113S bl113V zg112V csr12V te101S mw100T te100S mw102T me110T te103V ctr12V
+te102S qz11V zg120S zg121S me112T mw112T me120T me111T olV zg122S zg123V mw113T mw111T me121T mw110T me122T te111S qt20V
+my0T solY qz12V te112S te113V ye0V mw120T mw121T te110S mw122T me123T mw123T sc0Y te123S qt21V my1T sy0Y te121S te120V
+sc1Y te122V ye1V sy1Y qt22V my2T ss2S sc2Y ss3Y ye2V ss0S ss1S sy2Y
+"""
+
+Q4, U8, BF, F32, I32, U16 = "float8_e4m3fn_x4", "uint8", "bfloat16", "float32", "int32", "uint16"
+SCRATCH = {}
+
+
+def _sb(names, n, d):
+    for x in names.split():
+        SCRATCH[x] = ("sbuf", [128, n], d)
+
+
+_sb("xs z0 z1 t1 t2", 4 * C, BF)
+_sb("us vs", 512, BF)
+_sb("ds i16 jw a0 a1 a2", M, I32)
+_sb("ip pmi", 4, I32)
+_sb("pm pm1 corr", 4, F32)
+_sb("par0 t16 d0 d1 d2", 16, BF)
+_sb("wq qe", 512, Q4)
+_sb("wsc se", 512, U8)
+_sb("qu qu2 qv", 128, Q4)
+_sb("su su2 sv", 128, U8)
+_sb("gsel", 520, BF)
+_sb("qt0 qt1 qt2 qz0 qz1", C, Q4)
+_sb("st0 st1 st2 sz0 sz1", C, U8)
+_sb("lq0 lq1", H, Q4)
+_sb("ls0 ls1", H, U8)
+_sb("f0 f1", 4 * WW, BF)
+_sb("it cst", H + C, BF)
+_sb("w0 w1 e0 e1", WW, BF)
+_sb("pl", WW, F32)
+_sb("dd sg0 sg1 s0 s1", C, BF)
+_sb("rt0 rt1 tm1 tm2 tm3 tm4 tm5 tm6", C, "float16")
+_sb("olb yb", C, F32)
+_sb("uo", 8, U16)
+_sb("lp ln lk0 lk1 lk2 lk3 lk4 lk5 lk6 lr0 lr1", M, U16)
+for _b in range(8):
+    SCRATCH["ps%d" % _b] = ("psum", [128, 512], F32)
+
+LOADS = ["ldd", "ldu", "ldv", "ldw", "lds", "ldx0", "ldx1"]
+SEMAPHORES = ["cV", "cS", "cT", "cG", "arr0", "arr1", "sent", "outY", "outS"] + LOADS
+
+UNIT = 2.0 ** -11
+ZERO = B0 + H
+LIFT = 1280 * UNIT
+TINY = 1e-36
+
+
+def _cells(a):
+    return range(a[1], a[2], a[3] if len(a) > 3 else 1)
+
+
+def _meet(a, b):
+    if a[0] != b[0] or a[2] <= b[1] or b[2] <= a[1]:
+        return False
+    if len(a) < 4 and len(b) < 4:
+        return True
+    return not set(_cells(a)).isdisjoint(_cells(b))
+
+
+def plan(first, last, cfg):
+    A, F = AluOpType, ActivationFunctionType
+    K = cfg["K"]
+    ops = []
+
+    def ap(T, a):
+        if not isinstance(a, tuple):
+            return a
+        return T[a[0]][:, a[1]:a[2]:a[3]] if len(a) > 3 else T[a[0]][:, a[1]:a[2]]
+
+    def add(name, kind, n, engs, reads, writes, em, **kw):
+        o = {"name": name, "kind": kind, "n": n, "engs": engs, "r": reads, "w": writes, "em": em, "after": []}
+        o.update(kw)
+        ops.append(o)
+
+    def load(name, engs, out, src, rowb, codes=False):
+        def em(q, e, T, P):
+            d = ap(T, out)
+            return q.dma_start(d.bitcast(dt.uint8) if codes else d, src(T))
+        add(name, "load", rowb, engs, [], [out], em)
+
+    def store(name, reads, em, rowb):
+        add(name, "store", rowb, "YS", reads, [], em)
+
+    def iota(name, out, pattern, base, cm, whole=True):
+        def em(q, e, T, P):
+            if whole:
+                return q.iota(ap(T, out), pattern, base, cm)
+            return q.iota(ap(T, out), pattern, base, cm, allow_small_or_imprecise_dtypes=True)
+        add(name, "iota", out[2] - out[1], "G", [], [out], em)
+
+    def fill(name, out, c):
+        add(name, "fill", len(_cells(out)) // 2, "V", [], [out], lambda q, e, T, P: q.memset(ap(T, out), c))
+
+    def ts(name, out, in0, s1, s2, o0, o1=None):
+        def em(q, e, T, P):
+            if o1 is None:
+                return q.tensor_scalar(ap(T, out), ap(T, in0), ap(T, s1), None, o0)
+            return q.tensor_scalar(ap(T, out), ap(T, in0), ap(T, s1), ap(T, s2), o0, o1)
+        add(name, "ew", len(_cells(in0)), "V", [in0] + [s for s in (s1, s2) if isinstance(s, tuple)], [out], em, io=[in0, out])
+
+    def cp(name, out, in_, engs="V"):
+        def em(q, e, T, P):
+            if e == "S":
+                return q.activation(ap(T, out), ap(T, in_), F.Copy)
+            return q.tensor_copy(ap(T, out), ap(T, in_))
+        add(name, "ew", len(_cells(in_)), engs, [in_], [out], em, io=[in_, out])
+
+    def gather(name, out, win, a, b, lst):
+        off = (lst, a // 16, b // 16)
+
+        def em(q, e, T, P):
+            s = ap(T, win).indirect(ap(T, off))
+            if e == "S":
+                return q.activation(ap(T, out), s, F.Copy)
+            return q.tensor_copy(ap(T, out), s)
+        add(name, "gather", b - a, "SV", [win, off], [out], em)
+
+    def gmax(name, out, win, a, b, lst, in1):
+        off = (lst, a // 16, b // 16)
+        add(name, "gather", b - a, "V", [win, off, in1], [out],
+            lambda q, e, T, P: q.tensor_tensor(ap(T, out), ap(T, win).indirect(ap(T, off)), ap(T, in1), A.max))
+
+    def scan(name, out, d0, d1, init, o0, o1):
+        add(name, "ew", out[2] - out[1], "V", [d0, d1], [out],
+            lambda q, e, T, P: q.tensor_tensor_scan(ap(T, out), ap(T, d0), ap(T, d1), init, o0, o1), io=[d0, d1, out])
+
+    def tt(name, out, in0, in1, op):
+        add(name, "tt", out[2] - out[1], "V", [in0, in1], [out],
+            lambda q, e, T, P: q.tensor_tensor(ap(T, out), ap(T, in0), ap(T, in1), op))
+
+    def quant(name, cq, cs, a, b, src, a0):
+        i = (src, a0, a0 + 4 * (b - a))
+        add(name, "quant", b - a, "V", [i], [(cq, a, b), (cs, a, b)],
+            lambda q, e, T, P: q.quantize_mx(ap(T, (cq, a, b)), ap(T, (cs, a, b)), ap(T, i)))
+
+    def mm(name, tile, lq, ls, l0, rq, rs, a, b, start=True, stop=True, after=()):
+        rd = [(lq, l0, l0 + 128), (ls, l0, l0 + 128), (rq, a, b), (rs, a, b)]
+        add(name, "mm", b - a, "T", rd, [("#" + tile, 0, 1)],
+            lambda q, e, T, P: q.matmul_mx(P(tile, b - a), ap(T, rd[0]), ap(T, rd[1]), ap(T, rd[2]), ap(T, rd[3]), start, stop),
+            tile=tile, start=start, after=list(after))
+
+    def evac(name, out, tile, n, scale):
+        def em(q, e, T, P):
+            if e == "S":
+                return q.activation(ap(T, out), P(tile, n), F.Copy, scale=scale)
+            return q.tensor_scalar(ap(T, out), P(tile, n), scale, None, A.mult)
+        add(name, "ew", n, "SV", [("#" + tile, 0, 1)], [out], em, frees=tile)
+
+    def own(x, a, b):
+        return (x, B0 + a, B0 + b)
+
+    def upto(x, b):
+        return (x, 0, B0 + b)
+
+    def to_list(tag, lst, tmp, src, a, b):
+        scan("cs" + tag, (tmp, a, b), ("dd", a, b), own(src, a, b), 0.0, A.add, A.max)
+        ts("ct" + tag, (lst, a // 16, b // 16), (tmp, a + 15, b, 16), ("corr", 0, 1), 1.0 / UNIT, A.subtract, A.mult)
+
+    load("ldd", "YS", ("ds", 0, M), lambda T: T.dist[:, :], 4 * M)
+    load("ldu", "YS", ("us", 0, 512), lambda T: T.u[:, :], 1024)
+    for i, (a, b) in enumerate(cfg["TCH"][0]):
+        load("ldx%d" % i, "YS", ("xs", 4 * a, 4 * b), lambda T, a=a, b=b: T.x[:, 4 * a:4 * b], 8 * (b - a))
+    load("ldw", "Y", ("wq", 0, 512), lambda T: T.wc[:, :], 2048, codes=True)
+    load("lds", "Y", ("wsc", 0, 512), lambda T: T.ws[:, :], 512)
+    load("ldv", "Y", ("vs", 0, 512), lambda T: T.v[:, :], 1024)
+
+    iota("ip", ("ip", 0, 1), [[0, 1]], 0, 1)
+    iota("i16", ("i16", 0, M), [[16, M]], 0, 0)
+    iota("t16", ("t16", 0, 16), [[1, 16]], 0, 0, False)
+    iota("pl0", ("pl", 0, B0), [[1, H], [0, 4]], -H, 0, False)
+    iota("pl1", ("pl", B0, WW), [[1, C]], 0, 0, False)
+    fill("cs4", ("cst", 0, H), 2 * UNIT)
+    fill("cs1", ("cst", H, H + C), UNIT / 2)
+    scan("it0", ("it", 0, H), ("cst", 0, H), ("cst", 0, H), -(ZERO + 4) * UNIT, A.add, A.add)
+    scan("it1", ("it", H, H + C), ("cst", H, H + C), ("cst", H, H + C), -(H + 1) * UNIT, A.add, A.add)
+    fill("g64", ("gsel", 0, 516), 64.0)
+    add("sel", "iota", 516, "G", [("gsel", 0, 516)], [("gsel", 0, 516)],
+        lambda q, e, T, P: q.affine_select(T.gsel[:, 0:516], T.gsel[:, 0:516], [[1, 516]], A.is_equal, 0.0, -3, -4))
+    ts("pmi", ("pmi", 0, 1), ("ip", 0, 1), 15, None, A.bitwise_and)
+    cp("pm", ("pm", 0, 1), ("pmi", 0, 1))
+    ts("pm1", ("pm1", 0, 1), ("pm", 0, 1), 1.0, None, A.add)
+    ts("cor0", ("corr", 1, 2), ("pm", 0, 1), 15.0, LIFT, A.is_lt, A.mult)
+    ts("corr", ("corr", 0, 1), ("corr", 1, 2), -ZERO * UNIT, None, A.add)
+    ts("jw", ("jw", 0, M), ("i16", 0, M), ("pm", 0, 1), float(H), A.add, A.add)
+    ts("lp", ("lp", 0, M), ("i16", 0, M), 0.0, ("pm", 0, 1), A.mult, A.add)
+    cp("uo", ("uo", 0, 8), ("i16", 0, 8))
+    ts("d0", ("d0", 0, 16), ("t16", 0, 16), ("pm", 0, 1), -2.0, A.is_equal, A.mult)
+    ts("d1", ("d1", 0, 16), ("t16", 0, 16), ("pm1", 0, 1), LIFT, A.is_equal, A.mult)
+    tt("d2", ("d2", 0, 16), ("d0", 0, 16), ("d1", 0, 16), A.add)
+    gather("dd", ("dd", 0, C), ("d2", 0, 16), 0, C, "lp")
+    for x in ("w0", "w1", "e0", "e1"):
+        cp("h" + x, (x, 0, B0, 4), ("it", 0, H), "SV")
+    for b in range(4):
+        quant("qe%d" % b, "qe", "se", 128 * b, 128 * b + 128, "gsel", 3 - b)
+    quant("qu", "qu", "su", 0, 128, "us", 0)
+    add("pu", "gather", 128, "V", [("qu", 0, 128), ("uo", 0, 8)], [("qu2", 0, 128)],
+        lambda q, e, T, P: q.tensor_copy(T.qu2[:, 0:128].bitcast(dt.uint32), T.qu[:, 0:128].bitcast(dt.uint32).indirect(T.uo[:, 0:8])))
+    gather("pus", ("su2", 0, 128), ("su", 0, 128), 0, 128, "uo")
+    quant("qv", "qv", "sv", 0, 128, "vs", 0)
+    if first:
+        for t in range(ROUNDS):
+            for b in range(4):
+                fill("he%d%d" % (t, b), ("f%d" % t, WW * b, WW * b + B0, 4), 0.0)
+
+    tt("a0", ("a0", 0, M), ("jw", 0, M), ("ds", 0, M), A.subtract)
+    cp("ln", ("ln", 0, M), ("a0", 0, M))
+    ts("a1", ("a1", 0, M), ("a0", 0, M), float(H), 3.0, A.min, A.mult)
+    tt("a2", ("a2", 0, M), ("a0", 0, M), ("a1", 0, M), A.add)
+    cp("l0", ("lk0", 0, M), ("a2", 0, M))
+    for k in range(K + 1):
+        for i, (a, b) in enumerate(cfg["LCH"]):
+            if k == K:
+                a = max(a, 1 << K)
+            if k == 0:
+                gather("wg0%d" % i, own("w0", a, b), ("it", 0, H + b), a, b, "ln")
+                if a == 0:
+                    cp("par0", ("par0", 0, 1), own("w0", 0, 1), "SV")
+            else:
+                gather("wg%d%d" % (k, i), own("w%d" % (k % 2), a, b), upto("w%d" % ((k - 1) % 2), b), a, b, "lk%d" % (k - 1))
+                to_list("%d%d" % (k, i), "lk%d" % k, "tm%d" % k, "w%d" % (k % 2), a, b)
+
+    for i, (a, b) in enumerate(cfg["TCH"][0]):
+        quant("qt0%d" % i, "qt0", "st0", a, b, "xs", 4 * a)
+    for t in range(ROUNDS):
+        qt, st, ft, ee = "qt%d" % t, "st%d" % t, "f%d" % t, ["e0", "e1"]
+        halo = [(qt, C - H, C), (st, C - H, C)]
+        if not last:
+            add("snd%d" % t, "send", H, "G", halo, [], None, t=t)
+        if not first:
+            add("arr%d" % t, "arrive", H, "R", halo, [("lq%d" % t, 0, H), ("ls%d" % t, 0, H)], None, t=t,
+                after=[] if last else ["snd%d" % t])
+        for i, (a, b) in enumerate(cfg["TCH"][t]):
+            tile = "p%d%d" % (t, i)
+            mm("mp%d%d" % (t, i), tile, "qu2", "su2", 0, qt, st, a, b)
+            o = ("sg%d" % t, a, b)
+
+            def em(q, e, T, P, o=o, tile=tile):
+                if e == "S":
+                    return q.activation(ap(T, o), P(tile, o[2] - o[1]), F.Sign, bias=TINY)
+                return q.tensor_scalar(ap(T, o), P(tile, o[2] - o[1]), 0.0, 0.5, A.is_ge, A.subtract)
+            add("sg%d%d" % (t, i), "ew", b - a, "SV", [("#" + tile, 0, 1)], [o], em, frees=tile)
+            scan("fl%d%d" % (t, i), own("e0", a, b), ("it", H + a, H + b), o, -1.0, A.max, A.min)
+            if a == 0:
+                ts("fx%d" % t, own("e0", 0, 1), own("e0", 0, 1), ("par0", 0, 1), None, A.max)
+        for i, (a, b) in enumerate(cfg["FCH"][t]):
+            for p in range(4):
+                tile = "f%d%d%d" % (t, i, p)
+                mm("mf%d%d%d" % (t, i, p), tile, "qe", "se", 128 * p, qt, st, a, b)
+                evac("fe%d%d%d" % (t, i, p), (ft, WW * p + B0 + a, WW * p + B0 + b), tile, b - a, 1.0 / 64)
+        if not first:
+            for p in range(4):
+                tile = "h%d%d" % (t, p)
+                mm("mh%d%d" % (t, p), tile, "qe", "se", 128 * p, "lq%d" % t, "ls%d" % t, 0, H)
+                evac("he%d%d" % (t, p), (ft, WW * p, WW * p + B0, 4), tile, H, 1.0 / 64)
+        for k in range(K):
+            for i, (a, b) in enumerate(cfg["VCH"][t]):
+                sh = ("s%d" % (k % 2), a, b)
+                cp("sh%d%d%d" % (t, k, i), sh, own(ee[k % 2], a, b), "SV")
+                gmax("vs%d%d%d" % (t, k, i), own(ee[(k + 1) % 2], a, b), upto(ee[k % 2], b), a, b, "lk%d" % k, sh)
+        B, out, final = 1 << K, ee[K % 2], []
+        for n in range(1, (C - 1) // B + 1):
+            a, b = B * n, min(B * (n + 1), C)
+            gmax("bl%d%d" % (t, n), own(out, a, b), upto(out, a), a, b, "lk%d" % K, own(out, a, b))
+            for i, (a2, b2) in enumerate(cfg["TCH"][t + 1]):
+                if b2 <= b and i not in final:
+                    final.append(i)
+                    to_list("r%d%d" % (t, i), "lr%d" % t, "rt%d" % t, out, a2, b2)
+        z, qz, sz, tn = "z%d" % t, "qz%d" % t, "sz%d" % t, "t%d" % (t + 1)
+        for i, (a, b) in enumerate(cfg["TCH"][t + 1]):
+            g = "%d%d" % (t, i)
+            for p in range(4):
+                gather("zg%s%d" % (g, p), (z, 4 * a + p, 4 * b, 4), (ft, WW * p, WW * p + B0 + b), a, b, "lr%d" % t)
+            quant("qz" + g, qz, sz, a, b, z, 4 * a)
+            for p in range(4):
+                mm("me%s%d" % (g, p), "s%s%d" % (g, p), "qe", "se", 128 * p, qt, st, a, b, True, False, after=["zg%s0" % g])
+            for p in range(4):
+                mm("mw%s%d" % (g, p), "s%s%d" % (g, p), "wq", "wsc", 128 * p, qz, sz, a, b, False, True)
+                evac("te%s%d" % (g, p), (tn, 4 * a + p, 4 * b, 4), "s%s%d" % (g, p), b - a, 1.0 / 64)
+            quant("qt%d%d" % (t + 1, i), "qt%d" % (t + 1), "st%d" % (t + 1), a, b, tn, 4 * a)
+    gather("ol", ("olb", 0, C), ("pl", 0, WW), 0, C, "lr%d" % (ROUNDS - 1))
+    store("sol", [("olb", 0, C)], lambda q, e, T, P: q.dma_start(T.ol[:, :], T.olb[0:128:16, :]), 100)
+    for i, (a, b) in enumerate(cfg["TCH"][ROUNDS]):
+        mm("my%d" % i, "y%d" % i, "qv", "sv", 0, "qt2", "st2", a, b)
+        evac("ye%d" % i, ("yb", a, b), "y%d" % i, b - a, 1.0)
+        store("sy%d" % i, [("yb", a, b)], lambda q, e, T, P, a=a, b=b: q.dma_start(T.y[:, a:b], T.yb[:, a:b]), 4 * (b - a))
+        store("sc%d" % i, [("qt2", a, b)],
+              lambda q, e, T, P, a=a, b=b: q.dma_start(T.oc[:, 4 * a:4 * b], T.qt2[:, a:b].bitcast(dt.uint8)), 4 * (b - a))
+    for k in range(4):
+        store("ss%d" % k, [("st2", 0, C)],
+              lambda q, e, T, P, k=k: q.dma_start(T.osc[4 * k:4 * k + 4, :], T.st2[32 * k:32 * k + 4, :]), 100)
+
+    for j, o in enumerate(ops):
+        o["deps"] = [p["name"] for p in ops[:j]
+                     if any(_meet(a, b) for a in o["r"] + o["w"] for b in p["w"])
+                     or (p["kind"] != "arrive" and any(_meet(a, b) for a in o["w"] for b in p["r"]))]
+    return ops
+
+
+def emit(g, core, T, topo, ops, order, prev, nxt):
+    by = {o["name"]: o for o in ops}
+    seq = [(n, e if e in by[n]["engs"] else by[n]["engs"][0]) for n, e in order if n in by]
+    assert sorted(n for n, e in seq) == sorted(by)
+    queue = {"V": g.vector, "S": g.scalar, "T": g.tensor, "G": g, "Y": g.sync}
+    free, bank, waits = [(b, None) for b in range(8)], {}, {}
+    for n, e in seq:
+        o = by[n]
+        d = [] if o["kind"] == "arrive" else list(o["deps"])
+        if o.get("start"):
+            bank[o["tile"]], who = free.pop(0)
+            d += [who] if who else []
+        elif o["kind"] == "mm":
+            d = [x for x in d if by[x].get("tile") != o["tile"]]
+        if "frees" in o:
+            free.append((bank[o["frees"]], n))
+        waits[n] = d
+    needed = set(x for d in waits.values() for x in d)
+    total, done, known = {}, {}, {e: {} for e in queue}
+
+    def bump(s, k):
+        total[s] = total.get(s, 0) + k
+        return s, total[s]
+
+    for n, e in seq:
+        o = by[n]
+        if o["kind"] == "arrive":
+            done[n] = (bump(n, 2 * len(topo.engines(prev, core))), {})
+            continue
+        q, kn = queue[e], known[e]
+        want = {}
+        for x in waits[n]:
+            (s, k), clock = done[x]
+            if want.get(s, (0, None))[0] < k:
+                want[s] = (k, clock)
+        for s, (k, clock) in want.items():
+            if kn.get(s, 0) < k and not any(c.get(s, 0) >= k for s2, (k2, c) in want.items() if s2 != s):
+                q.wait_ge(T.sem[s], k)
+        for s, (k, clock) in want.items():
+            for s2, k2 in list(clock.items()) + [(s, k)]:
+                kn[s2] = max(kn.get(s2, 0), k2)
+        if o["kind"] == "send":
+            rid, pid, _ = topo.addr(nxt)
+            t, m = o["t"], topo.mask(core, nxt)
+            g.remote_dma(T["lq%d" % t][:, 0:H].bitcast(dt.uint8), T["qt%d" % t][:, C - H:C].bitcast(dt.uint8),
+                         T.sem["arr%d" % t], T.sem.sent, pid, rid, m)
+            g.remote_dma(T["ls%d" % t][:, 0:H], T["st%d" % t][:, C - H:C], T.sem["arr%d" % t], T.sem.sent, pid, rid, m)
+            bump("sent", 2 * len(topo.engines(core, nxt)))
+            continue
+        ins = o["em"](q, e, T, lambda tile, w: T["ps%d" % bank[tile]][:, 0:w])
+        if o["kind"] == "load":
+            ins.then_inc(T.sem[n], 16)
+            done[n] = (bump(n, 16), dict(kn))
+        elif o["kind"] == "store":
+            ins.then_inc(T.sem["out" + e], 16)
+            bump("out" + e, 16)
+        elif n in needed:
+            ins.then_inc(T.sem["c" + e], 1)
+            done[n] = (bump("c" + e, 1), dict(kn))
+    for s in ("sent", "outY", "outS"):
+        if s in total:
+            g.wait_ge(T.sem[s], total[s])
+
+
+def rank_program(g, core, T, topo):
+    rank = T.rank_of(core)
+    if rank is None:
+        return
+    prev = T.cores[rank - 1] if rank > 0 else None
+    nxt = T.cores[rank + 1] if rank + 1 < len(T.cores) else None
+    assert nxt is None or topo.may_write(core, nxt)
+    emit(g, core, T, topo, plan(prev is None, nxt is None, CFG), [(w[:-1], w[-1]) for w in ORDER.split()], prev, nxt)

@@ -5,25 +5,26 @@ M = C // 16
 B0 = 4 * H
 WW = B0 + C
 A1, A2, A3 = [(0, C)], [(0, C - H), (C - H, C)], [(0, 160), (160, 320), (320, C)]
-CFG = {"K": 5, "LCH": A2, "VCH": [A2, A2], "TCH": [A2, A2, A3], "FCH": [A1, A1]}
+CFG = {"K": 6, "LCH": A2, "VCH": [A2, A3], "TCH": [A2, A2, A3], "FCH": [A1, A1]}
 ORDER = """
-g64V cs4V cs1V lddY t16G ipG i16G pmiV pmV selG ldx1S d0V it0V lpV pm1V cor0V he1V jwV uoV d1V hw1V d2V it1V qe2V a0V
-hw0S lduY lnV a1V a2V ddS corrV l0V qe0V wg00S wg10S wg01V ldx0Y qt01V quV par0S cs10V ct10V wg11S cs11V puV pusS ct11V
-qt00V mp01T wg20S cs20V wg21S sg01S mp00T cs21V ct20V snd0G ct21V wg30V mf000T sg00S fl00V he0S fl01V fx0V wg31S cs30V
-qe1V cs31V ct30V sh000S vs000V mf002T sh001S arr0R vs001V mf001T wg40S sh010S sh011S cs40V fe002S mh02T ct31V ldsY mh01T
-vs010V vs011V sh021S sh020V mh00T ct40V vs020V wg41S vs021V sh030S qe3V wg50S vs030V sh031S cs41V mf003T cs50V vs031V
-ct50V sh040S fe001S mh03T ct41V wg51S vs040V sh041V bl01V he01S pl0G bl02V fe000S vs041V he00S he02S ldwY bl03V cs51V
-fe003S bl04V ct51V he03S bl05V bl06V bl07V bl08V csr00V bl09V ctr00V zg000S ldvY bl010V zg001S bl011V bl012V bl013V
-zg003V csr01V ctr01V me000T zg002S me001T qz00V zg010V me002T me011T me003T me012T me010T zg013S zg012S mw001T zg011V
-mw000T mw003T mw002T qz01V me013T te001S mw013T te000S te003S mw012T pl1G mw011T mw010T te013S te012S te002V qt10V mp10T
-te011V te010S sg10S qt11V mp11T snd1G fl10V mf101T fx1V mf103T sh100V sg11S fl11V vs100V sh101S mf100T vs101V sh110S
-arr1R mf102T vs110V sh111S sh120S vs111V mh10T sh121V vs120V mh13T vs121V fe102S sh130S sh131S fe100S qvV fe101S vs130V
-vs131V mh11T he13S sh140V he11S mh12T sh141V vs140V fe103S bl11V bl12V bl13V bl14V he10S bl15V he12S csr10V bl16V ctr10V
-zg103S zg100S vs141V bl17V zg102S bl18V bl19V csr11V me101T zg101S me100T bl110V ctr11V bl111V bl112V zg110S me113T
-me102T me103T zg111S qz10V mw103T mw101T zg113S bl113V zg112V csr12V te101S mw100T te100S mw102T me110T te103V ctr12V
-te102S qz11V zg120S zg121S me112T mw112T me120T me111T olV zg122S zg123V mw113T mw111T me121T mw110T me122T te111S qt20V
-my0T solY qz12V te112S te113V ye0V mw120T mw121T te110S mw122T me123T mw123T sc0Y te123S qt21V my1T sy0Y te121S te120V
-sc1Y te122V ye1V sy1Y qt22V my2T ss2S sc2Y ss3Y ye2V ss0S ss1S sy2Y
+lddY ipG cs1V pmiV it1V lduS ldx0S cs4V i16G pmV t16G g64V it0V pm1V he1S d0V jwV lpV d1V cor0V d2V pl1G uoV hw0S a0V
+corrV a1V ddS selG lnV qe0V a2V wg01V l0V quV wg00S ldx1Y hw1S wg10S pusS he0S wg11V puV cs11V par0S cs10V ct11V qt00V
+ct10V qe3V qt01V mp00T wg21S wg20S qe1V mp01T mf000T qe2V cs21V cs20V sg00S sg01S snd0G ct21V fx0V sh000V fl00V wg31S
+ct20V ldsY arr0R wg30S sh001V fl01V vs000V sh010S cs31V vs001V mf001T cs30V ct31V mf002T sh011S wg41S ct30V mf003T
+vs010V vs011V mh01T cs41V wg40S sh020V mh00T ldvY cs40V sh021S fe002S ct41V vs020V vs021V mh02T sh030V ct40V wg51S cs51V
+sh031S vs030V vs031V wg50S cs50V sh040S ct51V ct50V vs040V sh041S wg60S vs041V sh050V cs60V sh051S ldwY vs050V wg61S
+fe000S ct60V bl01V fe001S vs051V fe003S bl02V he01S cs61V bl03V ct61V csr00V he00S bl04V ctr00V mh03T bl05V zg000V
+me000T he02S he03S bl06V zg001V me001T csr01V zg002S zg003S ctr01V me003T qz00V zg010V zg013S me002T me010T zg012V
+mw000T mw001T mw003T zg011S qz01V mw002T me013T me011T te001S te000S me012T qvV mw011T te003S mw013T mw010T te002V qt10V
+te011S mw012T te013S mp10T te012S sg10S pl0G te010V qt11V fl10V mp11T sh100V fx1V sg11S fl11V mf101T sh101V sh102V
+vs100V vs101V snd1G sh110S vs102V sh111V vs110V vs111V sh112S sh120S mf103T sh121S vs112V vs120V sh122S fe101S mf102T
+arr1R vs121V sh130S vs122V sh131S vs130V vs131V sh132S mf100T mh11T sh140S vs132V sh141V sh142S fe100S vs140V mh12T
+sh150S mh13T vs141V sh151S vs142V vs150V vs151V sh152S bl11V fe102S fe103S he11S bl12V he12S vs152V mh10T bl13V he13S
+he10S csr10V bl14V ctr10V csr11V bl15V zg103V zg101S zg100S zg102S ctr11V me101T bl16V zg110V csr12V me102T me103T
+me100T qz10V me113T mw102T ctr12V mw103T zg112V mw100T mw101T zg113S zg111S me110T zg123S me112T zg122V qz11V te102V
+zg121S te103V me111T zg120S mw112T te100S mw111T mw110T me121T me123T te101V me122T olS qz12V mw113T qt20V mw122T te112V
+sc0Y te111S my0T te110V mw121T te113S ye0V mw123T qt21V me120T te122S solY te123S sy0Y mw120T te120V te121S my1T sc1Y
+qt22V my2T sc2S ye1V ye2V ss1S ss0Y sy1Y ss3S ss2Y sy2Y
 """
 
 Q4, U8, BF, F32, I32, U16 = "float8_e4m3fn_x4", "uint8", "bfloat16", "float32", "int32", "uint16"
@@ -147,8 +148,8 @@ def plan(first, last, cfg):
             lambda q, e, T, P: q.tensor_tensor(ap(T, out), ap(T, win).indirect(ap(T, off)), ap(T, in1), A.max))
 
     def scan(name, out, d0, d1, init, o0, o1):
-        add(name, "ew", out[2] - out[1], "V", [d0, d1], [out],
-            lambda q, e, T, P: q.tensor_tensor_scan(ap(T, out), ap(T, d0), ap(T, d1), init, o0, o1), io=[d0, d1, out])
+        add(name, "ew", out[2] - out[1], "V", [d0, d1] + ([init] if isinstance(init, tuple) else []), [out],
+            lambda q, e, T, P: q.tensor_tensor_scan(ap(T, out), ap(T, d0), ap(T, d1), ap(T, init), o0, o1), io=[d0, d1, out])
 
     def tt(name, out, in0, in1, op):
         add(name, "tt", out[2] - out[1], "V", [in0, in1], [out],
@@ -265,9 +266,9 @@ def plan(first, last, cfg):
                     return q.activation(ap(T, o), P(tile, o[2] - o[1]), F.Sign, bias=TINY)
                 return q.tensor_scalar(ap(T, o), P(tile, o[2] - o[1]), 0.0, 0.5, A.is_ge, A.subtract)
             add("sg%d%d" % (t, i), "ew", b - a, "SV", [("#" + tile, 0, 1)], [o], em, frees=tile)
-            scan("fl%d%d" % (t, i), own("e0", a, b), ("it", H + a, H + b), o, -1.0, A.max, A.min)
+            scan("fl%d%d" % (t, i), own("e0", max(a, 1), b), ("it", H + max(a, 1), H + b), (o[0], max(a, 1), b), -1.0, A.max, A.min)
             if a == 0:
-                ts("fx%d" % t, own("e0", 0, 1), own("e0", 0, 1), ("par0", 0, 1), None, A.max)
+                scan("fx%d" % t, own("e0", 0, 1), (o[0], 0, 1), ("it", H, H + 1), ("par0", 0, 1), A.max, A.min)
         for i, (a, b) in enumerate(cfg["FCH"][t]):
             for p in range(4):
                 tile = "f%d%d%d" % (t, i, p)
@@ -281,7 +282,10 @@ def plan(first, last, cfg):
         for k in range(K):
             for i, (a, b) in enumerate(cfg["VCH"][t]):
                 sh = ("s%d" % (k % 2), a, b)
-                cp("sh%d%d%d" % (t, k, i), sh, own(ee[k % 2], a, b), "SV")
+                if k == 0:
+                    scan("sh%d0%d" % (t, i), sh, ("it", H + a, H + b), ("sg%d" % t, a, b), -1.0, A.max, A.min)
+                else:
+                    cp("sh%d%d%d" % (t, k, i), sh, own(ee[k % 2], a, b), "SV")
                 gmax("vs%d%d%d" % (t, k, i), own(ee[(k + 1) % 2], a, b), upto(ee[k % 2], b), a, b, "lk%d" % k, sh)
         B, out, final = 1 << K, ee[K % 2], []
         for n in range(1, (C - 1) // B + 1):

@@ -5,26 +5,29 @@ M = C // 16
 B0 = 4 * H
 WW = B0 + C
 A1, A2, A3 = [(0, C)], [(0, C - H), (C - H, C)], [(0, 160), (160, 320), (320, C)]
-CFG = {"K": 6, "LCH": A2, "VCH": [A2, A3], "TCH": [A2, A2, A3], "FCH": [A1, A1]}
+CFG = {"K": 6, "LCH": A3, "VCH": [A3, A3], "TCH": [A2, A3, A3], "FCH": [A1, A1]}
 ORDER = """
-lddY ipG cs1V pmiV it1V lduS ldx0S cs4V i16G pmV t16G g64V it0V pm1V he1S d0V jwV lpV d1V cor0V d2V pl1G uoV hw0S a0V
-corrV a1V ddS selG lnV qe0V a2V wg01V l0V quV wg00S ldx1Y hw1S wg10S pusS he0S wg11V puV cs11V par0S cs10V ct11V qt00V
-ct10V qe3V qt01V mp00T wg21S wg20S qe1V mp01T mf000T qe2V cs21V cs20V sg00S sg01S snd0G ct21V fx0V sh000V fl00V wg31S
-ct20V ldsY arr0R wg30S sh001V fl01V vs000V sh010S cs31V vs001V mf001T cs30V ct31V mf002T sh011S wg41S ct30V mf003T
-vs010V vs011V mh01T cs41V wg40S sh020V mh00T ldvY cs40V sh021S fe002S ct41V vs020V vs021V mh02T sh030V ct40V wg51S cs51V
-sh031S vs030V vs031V wg50S cs50V sh040S ct51V ct50V vs040V sh041S wg60S vs041V sh050V cs60V sh051S ldwY vs050V wg61S
-fe000S ct60V bl01V fe001S vs051V fe003S bl02V he01S cs61V bl03V ct61V csr00V he00S bl04V ctr00V mh03T bl05V zg000V
-me000T he02S he03S bl06V zg001V me001T csr01V zg002S zg003S ctr01V me003T qz00V zg010V zg013S me002T me010T zg012V
-mw000T mw001T mw003T zg011S qz01V mw002T me013T me011T te001S te000S me012T qvV mw011T te003S mw013T mw010T te002V qt10V
-te011S mw012T te013S mp10T te012S sg10S pl0G te010V qt11V fl10V mp11T sh100V fx1V sg11S fl11V mf101T sh101V sh102V
-vs100V vs101V snd1G sh110S vs102V sh111V vs110V vs111V sh112S sh120S mf103T sh121S vs112V vs120V sh122S fe101S mf102T
-arr1R vs121V sh130S vs122V sh131S vs130V vs131V sh132S mf100T mh11T sh140S vs132V sh141V sh142S fe100S vs140V mh12T
-sh150S mh13T vs141V sh151S vs142V vs150V vs151V sh152S bl11V fe102S fe103S he11S bl12V he12S vs152V mh10T bl13V he13S
-he10S csr10V bl14V ctr10V csr11V bl15V zg103V zg101S zg100S zg102S ctr11V me101T bl16V zg110V csr12V me102T me103T
-me100T qz10V me113T mw102T ctr12V mw103T zg112V mw100T mw101T zg113S zg111S me110T zg123S me112T zg122V qz11V te102V
-zg121S te103V me111T zg120S mw112T te100S mw111T mw110T me121T me123T te101V me122T olS qz12V mw113T qt20V mw122T te112V
-sc0Y te111S my0T te110V mw121T te113S ye0V mw123T qt21V me120T te122S solY te123S sy0Y mw120T te120V te121S my1T sc1Y
-qt22V my2T sc2S ye1V ye2V ss1S ss0Y sy1Y ss3S ss2Y sy2Y
+ipG cs1V pmiV t16G lddS i16G g64V pmV cs4V selG it1V d0V pm1V d1V ldx1Y jwV lpV it0V d2V cor0V ddS lduY corrV a0V hw2V
+hw0V a1V lnV a2V wg01S wg00V l0V ldx0Y wg02S qt01V wg10S wg11V wg12S qe3V cs11V hw1S cs10V he1S cs12V ct11V wg21S ct10V
+quV uoV ct12V pusS par0S wg20V puV mp01T cs21V cs20V qt00V wg22S ct20V ct21V he0S cs22V qe0V wg31S mp00T wg30V ct22V
+sg00S sg01S cs30V qe2V cs31V ct30V fx0V wg32S wg40S he2S fl00V sh000V ct31V pl0G fl01V cs32V vs000V wg41S snd0G arr0R
+sh001V mf003T cs40V sh002V sh010S ct32V wg42S pl1G vs001V sh011S cs41V vs010V ldwY mf002T sh020S ct41V ct40V wg51S
+vs002V cs42V vs011V sh012V vs020V vs012V wg50S sh021S ct42V fe003S ldsY sh030S cs51V cs50V vs021V mf000T qe1V mf001T
+mh01T mh02T mh03T sh022S ct50V wg52S ct51V sh031V wg60S vs030V vs031V wg61S sh040S cs52V vs022V sh041V cs60V fe002S
+ct52V cs61V sh032S vs040V wg62S vs041V mh00T sh050S vs032V cs62V ldvY ct60V ct61V sh051S vs050V sh042S vs051V bl01V
+vs042V bl02V fe000S he01S he02S he00S sh052V he03S csr00V bl03V fe001S vs052V ctr00V zg000S bl04V me000T me001T ct62V
+csr01V bl05V zg003S zg001V ctr01V zg002S bl06V me003T csr02V zg010S qz00V me002T me011T zg012S ctr02V me010T mw001T
+zg013S mw000T me012T zg011V mw003T mw002T zg020S zg022V te000S te003S zg023S me013T qz01V te001V te002V zg021V mw010T
+qt10V mw011T mw012T me020T mw013T me023T te010S qz02V me022T te013V te011S me021T mp10T mw022T qvV te012S mw020T sg10S
+qt11V te020V mw023T te022S te023S mw021T te021V fl10V mp11T sg11S sh100V fx1V qt12V vs100V mp12T sg12S sh101V fl11V
+sh110V vs101V sh102V fl12V snd1G sh111S vs110V arr1R vs102V sh120V vs111V vs120V mf100T sh121V sh112S sh130S mf103T
+vs112V mf101T sh122S vs121V vs130V vs122V mf102T sh131S sh140V fe101S vs131V vs140V sh141V sh132S fe103S vs132V sh150S
+fe100S vs141V sh142S mh13T sh151V vs150V vs151V bl11V vs142V bl12V sh152V mh11T bl13V csr10V mh10T vs152V bl14V fe102S
+mh12T ctr10V he10V he13S csr11V bl15V zg100V he11S he12S me101T zg101S zg102S ctr11V zg110S bl16V me112T zg103V me110T
+me103T me100T csr12V zg111V zg113S me111T ctr12V qz10V me113T zg121V me102T mw100T zg112S mw101T qz11V mw103T mw102T olS
+mw110T zg120S solY mw112T mw113T mw111T zg123V zg122V te101V te103S me123T te100V me122T te102S me121T qz12V te113V
+te110S te112S me120T mw122T qt20V te111S mw123T sc0S mw120T te122S mw121T te120S qt21V my0T te123V te121V sc1S ye0V
+qt22V my1T sy0Y sc2Y ye1V ss1S my2T ss0S ye2V sy1S sy2Y ss2Y ss3Y
 """
 
 Q4, U8, BF, F32, I32, U16 = "float8_e4m3fn_x4", "uint8", "bfloat16", "float32", "int32", "uint16"
@@ -53,7 +56,7 @@ _sb("lq0 lq1", H, Q4)
 _sb("ls0 ls1", H, U8)
 _sb("f0 f1", 4 * WW, BF)
 _sb("it cst", H + C, BF)
-_sb("w0 w1 e0 e1", WW, BF)
+_sb("w0 w1 w2 e0 e1 e2", WW, BF)
 _sb("pl", WW, F32)
 _sb("dd sg0 sg1 s0 s1", C, BF)
 _sb("rt0 rt1 tm1 tm2 tm3 tm4 tm5 tm6", C, "float16")
@@ -215,7 +218,7 @@ def plan(first, last, cfg):
     ts("d1", ("d1", 0, 16), ("t16", 0, 16), ("pm1", 0, 1), LIFT, A.is_equal, A.mult)
     tt("d2", ("d2", 0, 16), ("d0", 0, 16), ("d1", 0, 16), A.add)
     gather("dd", ("dd", 0, C), ("d2", 0, 16), 0, C, "lp")
-    for x in ("w0", "w1", "e0", "e1"):
+    for x in ("w0", "w1", "w2", "e0", "e1", "e2"):
         cp("h" + x, (x, 0, B0, 4), ("it", 0, H), "SV")
     for b in range(4):
         quant("qe%d" % b, "qe", "se", 128 * b, 128 * b + 128, "gsel", 3 - b)
@@ -243,13 +246,13 @@ def plan(first, last, cfg):
                 if a == 0:
                     cp("par0", ("par0", 0, 1), own("w0", 0, 1), "SV")
             else:
-                gather("wg%d%d" % (k, i), own("w%d" % (k % 2), a, b), upto("w%d" % ((k - 1) % 2), b), a, b, "lk%d" % (k - 1))
-                to_list("%d%d" % (k, i), "lk%d" % k, "tm%d" % k, "w%d" % (k % 2), a, b)
+                gather("wg%d%d" % (k, i), own("w%d" % (k % 3), a, b), upto("w%d" % ((k - 1) % 3), b), a, b, "lk%d" % (k - 1))
+                to_list("%d%d" % (k, i), "lk%d" % k, "tm%d" % k, "w%d" % (k % 3), a, b)
 
     for i, (a, b) in enumerate(cfg["TCH"][0]):
         quant("qt0%d" % i, "qt0", "st0", a, b, "xs", 4 * a)
     for t in range(ROUNDS):
-        qt, st, ft, ee = "qt%d" % t, "st%d" % t, "f%d" % t, ["e0", "e1"]
+        qt, st, ft, ee = "qt%d" % t, "st%d" % t, "f%d" % t, ["e0", "e1", "e2"]
         halo = [(qt, C - H, C), (st, C - H, C)]
         if not last:
             add("snd%d" % t, "send", H, "G", halo, [], None, t=t)
@@ -285,9 +288,9 @@ def plan(first, last, cfg):
                 if k == 0:
                     scan("sh%d0%d" % (t, i), sh, ("it", H + a, H + b), ("sg%d" % t, a, b), -1.0, A.max, A.min)
                 else:
-                    cp("sh%d%d%d" % (t, k, i), sh, own(ee[k % 2], a, b), "SV")
-                gmax("vs%d%d%d" % (t, k, i), own(ee[(k + 1) % 2], a, b), upto(ee[k % 2], b), a, b, "lk%d" % k, sh)
-        B, out, final = 1 << K, ee[K % 2], []
+                    cp("sh%d%d%d" % (t, k, i), sh, own(ee[k % 3], a, b), "SV")
+                gmax("vs%d%d%d" % (t, k, i), own(ee[(k + 1) % 3], a, b), upto(ee[k % 3], b), a, b, "lk%d" % k, sh)
+        B, out, final = 1 << K, ee[K % 3], []
         for n in range(1, (C - 1) // B + 1):
             a, b = B * n, min(B * (n + 1), C)
             gmax("bl%d%d" % (t, n), own(out, a, b), upto(out, a), a, b, "lk%d" % K, own(out, a, b))

@@ -2,32 +2,37 @@ from concourse.mybir import dt, AluOpType, ActivationFunctionType
 
 C, H, ROUNDS = 448, 192, 2
 M = C // 16
-B0 = 4 * H
-WW = B0 + C
-A1, A2, A3 = [(0, C)], [(0, C - H), (C - H, C)], [(0, 160), (160, 320), (320, C)]
-CFG = {"K": 6, "LCH": A3, "VCH": [A3, A3], "TCH": [A2, A3, A3], "FCH": [A1, A1]}
+WW = H + C
+RADIX, LEVELS = 4, 3
+W = C // RADIX
+BLK = RADIX ** LEVELS
+NB = C // BLK
+CFG = {"RUNS": [(0, 192), (192, 448)], "XCH": [(0, 192), (192, 448)],
+       "TCH": [[(0, 192), (192, 320), (320, 448)], [(0, 192), (192, 320), (320, 448)]],
+       "FCH": [[(0, 448)], [(0, 448)]], "PCH": [(0, 192), (192, 448)], "SND": [[(256, 448)], [(256, 448)]],
+       "CT": [(1, 4)], "CF": [(0, 3), (3, 7)], "SB": [None, None], "ZB": [None, None], "PB": [None, None],
+       "LORD": ["u", "x0", "x1"]}
 ORDER = """
-ipG cs1V pmiV t16G lddS i16G g64V pmV cs4V selG it1V d0V pm1V d1V ldx1Y jwV lpV it0V d2V cor0V ddS lduY corrV a0V hw2V
-hw0V a1V lnV a2V wg01S wg00V l0V ldx0Y wg02S qt01V wg10S wg11V wg12S qe3V cs11V hw1S cs10V he1S cs12V ct11V wg21S ct10V
-quV uoV ct12V pusS par0S wg20V puV mp01T cs21V cs20V qt00V wg22S ct20V ct21V he0S cs22V qe0V wg31S mp00T wg30V ct22V
-sg00S sg01S cs30V qe2V cs31V ct30V fx0V wg32S wg40S he2S fl00V sh000V ct31V pl0G fl01V cs32V vs000V wg41S snd0G arr0R
-sh001V mf003T cs40V sh002V sh010S ct32V wg42S pl1G vs001V sh011S cs41V vs010V ldwY mf002T sh020S ct41V ct40V wg51S
-vs002V cs42V vs011V sh012V vs020V vs012V wg50S sh021S ct42V fe003S ldsY sh030S cs51V cs50V vs021V mf000T qe1V mf001T
-mh01T mh02T mh03T sh022S ct50V wg52S ct51V sh031V wg60S vs030V vs031V wg61S sh040S cs52V vs022V sh041V cs60V fe002S
-ct52V cs61V sh032S vs040V wg62S vs041V mh00T sh050S vs032V cs62V ldvY ct60V ct61V sh051S vs050V sh042S vs051V bl01V
-vs042V bl02V fe000S he01S he02S he00S sh052V he03S csr00V bl03V fe001S vs052V ctr00V zg000S bl04V me000T me001T ct62V
-csr01V bl05V zg003S zg001V ctr01V zg002S bl06V me003T csr02V zg010S qz00V me002T me011T zg012S ctr02V me010T mw001T
-zg013S mw000T me012T zg011V mw003T mw002T zg020S zg022V te000S te003S zg023S me013T qz01V te001V te002V zg021V mw010T
-qt10V mw011T mw012T me020T mw013T me023T te010S qz02V me022T te013V te011S me021T mp10T mw022T qvV te012S mw020T sg10S
-qt11V te020V mw023T te022S te023S mw021T te021V fl10V mp11T sg11S sh100V fx1V qt12V vs100V mp12T sg12S sh101V fl11V
-sh110V vs101V sh102V fl12V snd1G sh111S vs110V arr1R vs102V sh120V vs111V vs120V mf100T sh121V sh112S sh130S mf103T
-vs112V mf101T sh122S vs121V vs130V vs122V mf102T sh131S sh140V fe101S vs131V vs140V sh141V sh132S fe103S vs132V sh150S
-fe100S vs141V sh142S mh13T sh151V vs150V vs151V bl11V vs142V bl12V sh152V mh11T bl13V csr10V mh10T vs152V bl14V fe102S
-mh12T ctr10V he10V he13S csr11V bl15V zg100V he11S he12S me101T zg101S zg102S ctr11V zg110S bl16V me112T zg103V me110T
-me103T me100T csr12V zg111V zg113S me111T ctr12V qz10V me113T zg121V me102T mw100T zg112S mw101T qz11V mw103T mw102T olS
-mw110T zg120S solY mw112T mw113T mw111T zg123V zg122V te101V te103S me123T te100V me122T te102S me121T qz12V te113V
-te110S te112S me120T mw122T qt20V te111S mw123T sc0S mw120T te122S mw121T te120S qt21V my0T te123V te121V sc1S ye0V
-qt22V my1T sy0Y sc2Y ye1V ss1S my2T ss0S ye2V sy1S sy2Y ss2Y ss3Y
+lddS lduY ldx0Y rrG ipG nt21G i16G xdV cstV tmd0V edV qiV nt30G it0V qfV val10S nt20G g64V jwV d1S d0S nt31G val21S
+hrbS uoV ldx1Y val20S lpV a0V d2V val11V lnV cwV quV dd1V it1S corrS selG par0S ddV puV xs110V xs120V par1S xs130V
+qe2V qt00V xc10S val31S xl110V xs131V xs111V val30S pusS xs121V mp00T dd2V x110V xl111V xc11S dd3V x120V ea000V qt01V
+x130V x111V eb00V xc20S ldwY xs220V xs210V xs230V mp01T x121V e0110V xl210V ea011V x131V snd00G ldsY e0120V x210V
+eb01V x220V e0130V xs211V e0111V x230V xs221V xs231V qe3V e0121V xs320V mf002T arr00R fe002S xc21S ldvY e0c20S xl211V
+xs330V xs310V e0210V e0131V x211V xl310V xc30S e0220V qe1V e0c21S x221V x310V e0230V x231V x320V mf001T e0211V e0c30S
+xc31S xs321V xs331V xs311V x330V e0310V mf003T fe003S e0221V mh01T xl311V xf1V xf2V xf0V e0320V x311V e0231V lf0V
+e0330V x321V mh03T qe0V mh00T bl00V x331V e0c31S e0311V he03S fe001S he01S bl01V he00S mh02T mf000T xf4V xf5V he02S
+e0321V xf3V xf6V bl02V e0331V lf3V rs00V rs01V rs02V bl03V fe000S me013T qvV rl00V bl04V me011T rs03V me010T zg003V
+rs04V bl05V me003T zg000S zg002V me001T zg001S bl06V rs05V rl01V qz00V rs06V me000T me012T me002T mw001T zg011S zg013V
+rl02V zg012V zg010S zg021V te001S mw000T mw002T mw003T qz01V me020T te000S te002S te003S zg023V zg020V mw010T mw011T
+zg022S te010S me021T mw013T qt10V qz02V me022T mw012T me023T mp10T te012V te011S eb10V te013S mw022T te022S ea100V
+mw023T mw020T qt11V te023S mw021T te020S mp11T te021V e1110V qt12V snd10G e1120V eb11V e1130V e1c20S mp12T eb12V
+mf100T ea111V ea121V e1210V mf102T mf103T e1111V e1220V e1121V e1230V e1c30S e1131V arr10R mf101T mh12T e1310V e1c21S
+fe101S fe100S mh10T mh11T e1211V fe103S e1320V e1221V e1330V mh13T fe102S he10S e1231V bl10V e1c31V bl11V e1311V he11S
+he13S he12S me111T bl12V e1321V me100T me102T me101T rs11V rs10V rs12V e1331V rl10V zg100S bl13V zg101V rs13V me121T
+me112T bl14V zg102S zg103V rs14V bl15V rl11V me103T qz10V zg110S zg112S me110T zg113V bl16V zg111V mw100T mw102T
+mw103T rs15V rs16V te100S qz11V te102S olS rl12V zg121S mw101T me113T te103V mw112T te101V mw111T me123T solY zg123S
+te111S zg122V zg120V qt20V mw110T te112V mw113T me120T te110S me122T qz12V my0T mw121T te113S qt21V sc0Y ye0V mw123T
+mw120T te121S te120S mw122T te123V my1T te122V sc1Y sy0Y qt22V ye1S sy1S sc2Y my2T ss3Y ss2S ss0S ss1S ye2S sy2Y
 """
 
 Q4, U8, BF, F32, I32, U16 = "float8_e4m3fn_x4", "uint8", "bfloat16", "float32", "int32", "uint16"
@@ -41,10 +46,12 @@ def _sb(names, n, d):
 
 _sb("xs z0 z1 t1 t2", 4 * C, BF)
 _sb("us vs", 512, BF)
-_sb("ds i16 jw a0 a1 a2", M, I32)
-_sb("ip pmi", 4, I32)
-_sb("pm pm1 corr", 4, F32)
-_sb("par0 t16 d0 d1 d2", 16, BF)
+_sb("ds a0", M, I32)
+_sb("i16 jw", M, F32)
+_sb("ip qi", 32, I32)
+_sb("qf", 32, F32)
+_sb("corr d0 d1 d2", 16, F32)
+_sb("cw", W, F32)
 _sb("wq qe", 512, Q4)
 _sb("wsc se", 512, U8)
 _sb("qu qu2 qv", 128, Q4)
@@ -55,24 +62,27 @@ _sb("st0 st1 st2 sz0 sz1", C, U8)
 _sb("lq0 lq1", H, Q4)
 _sb("ls0 ls1", H, U8)
 _sb("f0 f1", 4 * WW, BF)
-_sb("it cst", H + C, BF)
-_sb("w0 w1 w2 e0 e1 e2", WW, BF)
-_sb("pl", WW, F32)
-_sb("dd sg0 sg1 s0 s1", C, BF)
-_sb("rt0 rt1 tm1 tm2 tm3 tm4 tm5 tm6", C, "float16")
-_sb("olb yb", C, F32)
+_sb("cst", WW // 2, BF)
+_sb("it rb", WW, F32)
+_sb("xb eb", 2400, F32)
+_sb("nt val ddk", W * LEVELS, F32)
+_sb("dd", BLK, F32)
+_sb("tm", 1600, F32)
+_sb("tf rt0 rt1 olb yb", C, F32)
 _sb("uo", 8, U16)
-_sb("lp ln lk0 lk1 lk2 lk3 lk4 lk5 lk6 lr0 lr1", M, U16)
+_sb("lp", 16, U16)
+_sb("ll", 100, U16)
+_sb("ln lf lr0 lr1", M, U16)
 for _b in range(8):
     SCRATCH["ps%d" % _b] = ("psum", [128, 512], F32)
 
-LOADS = ["ldd", "ldu", "ldv", "ldw", "lds", "ldx0", "ldx1"]
-SEMAPHORES = ["cV", "cS", "cT", "cG", "arr0", "arr1", "sent", "outY", "outS"] + LOADS
+LOADS = ["ldd", "ldu", "ldv", "ldw", "lds", "ldx0", "ldx1", "ldx2"]
+SEMAPHORES = ["cV", "cS", "cT", "cG", "arr00", "arr10", "arr01", "arr11", "sent", "outY", "outS"] + LOADS
 
-UNIT = 2.0 ** -11
-ZERO = B0 + H
-LIFT = 1280 * UNIT
-TINY = 1e-36
+UNIT = 2.0 ** -92
+LIFT = 2048 * UNIT
+DROP = 4096 * UNIT
+LABEL = [None]
 
 
 def _cells(a):
@@ -89,7 +99,6 @@ def _meet(a, b):
 
 def plan(first, last, cfg):
     A, F = AluOpType, ActivationFunctionType
-    K = cfg["K"]
     ops = []
 
     def ap(T, a):
@@ -97,230 +106,285 @@ def plan(first, last, cfg):
             return a
         return T[a[0]][:, a[1]:a[2]:a[3]] if len(a) > 3 else T[a[0]][:, a[1]:a[2]]
 
-    def add(name, kind, n, engs, reads, writes, em, **kw):
-        o = {"name": name, "kind": kind, "n": n, "engs": engs, "r": reads, "w": writes, "em": em, "after": []}
+    def add(name, kind, engs, reads, writes, em, **kw):
+        o = {"name": name, "kind": kind, "engs": engs, "r": reads, "w": writes, "em": em, "after": []}
         o.update(kw)
         ops.append(o)
 
-    def load(name, engs, out, src, rowb, codes=False):
+    def load(name, engs, out, src, codes=False, behind=(), after=()):
         def em(q, e, T, P):
             d = ap(T, out)
             return q.dma_start(d.bitcast(dt.uint8) if codes else d, src(T))
-        add(name, "load", rowb, engs, [], [out], em)
+        add(name, "load", engs, list(behind), [out], em, after=list(after))
 
-    def store(name, reads, em, rowb):
-        add(name, "store", rowb, "YS", reads, [], em)
+    def store(name, reads, em):
+        add(name, "store", "YS", reads, [], em)
 
     def iota(name, out, pattern, base, cm, whole=True):
         def em(q, e, T, P):
             if whole:
                 return q.iota(ap(T, out), pattern, base, cm)
             return q.iota(ap(T, out), pattern, base, cm, allow_small_or_imprecise_dtypes=True)
-        add(name, "iota", out[2] - out[1], "G", [], [out], em)
+        add(name, "iota", "G", [], [out], em)
 
     def fill(name, out, c):
-        add(name, "fill", len(_cells(out)) // 2, "V", [], [out], lambda q, e, T, P: q.memset(ap(T, out), c))
+        add(name, "fill", "V", [], [out], lambda q, e, T, P: q.memset(ap(T, out), c))
 
     def ts(name, out, in0, s1, s2, o0, o1=None):
         def em(q, e, T, P):
             if o1 is None:
                 return q.tensor_scalar(ap(T, out), ap(T, in0), ap(T, s1), None, o0)
             return q.tensor_scalar(ap(T, out), ap(T, in0), ap(T, s1), ap(T, s2), o0, o1)
-        add(name, "ew", len(_cells(in0)), "V", [in0] + [s for s in (s1, s2) if isinstance(s, tuple)], [out], em, io=[in0, out])
+        add(name, "ew", "V", [in0] + [s for s in (s1, s2) if isinstance(s, tuple)], [out], em)
+
+    def lin(name, out, in_, scale, bias):
+        def em(q, e, T, P):
+            if e == "S":
+                return q.activation(ap(T, out), ap(T, in_), F.Identity, bias=ap(T, bias), scale=scale)
+            return q.tensor_scalar(ap(T, out), ap(T, in_), scale, ap(T, bias), A.mult, A.add)
+        add(name, "ew", "SV", [in_] + ([bias] if isinstance(bias, tuple) else []), [out], em)
+
+    def flag(name, out, in_, end, way, size):
+        def em(q, e, T, P):
+            if e == "S":
+                return q.activation(ap(T, out), ap(T, in_), F.Relu, bias=size * (1.0 - way * end), scale=size * way)
+            return q.tensor_scalar(ap(T, out), ap(T, in_), end, size, A.is_equal, A.mult)
+        add(name, "ew", "SV", [in_], [out], em)
 
     def cp(name, out, in_, engs="V"):
         def em(q, e, T, P):
             if e == "S":
                 return q.activation(ap(T, out), ap(T, in_), F.Copy)
             return q.tensor_copy(ap(T, out), ap(T, in_))
-        add(name, "ew", len(_cells(in_)), engs, [in_], [out], em, io=[in_, out])
+        add(name, "ew", engs, [in_], [out], em)
 
-    def gather(name, out, win, a, b, lst):
-        off = (lst, a // 16, b // 16)
-
+    def gather(name, out, win, off):
         def em(q, e, T, P):
             s = ap(T, win).indirect(ap(T, off))
             if e == "S":
                 return q.activation(ap(T, out), s, F.Copy)
             return q.tensor_copy(ap(T, out), s)
-        add(name, "gather", b - a, "SV", [win, off], [out], em)
+        add(name, "gather", "SV", [win, off], [out], em)
 
-    def gmax(name, out, win, a, b, lst, in1):
-        off = (lst, a // 16, b // 16)
-        add(name, "gather", b - a, "V", [win, off, in1], [out],
-            lambda q, e, T, P: q.tensor_tensor(ap(T, out), ap(T, win).indirect(ap(T, off)), ap(T, in1), A.max))
+    def gtt(name, out, win, off, in1, op):
+        add(name, "gather", "V", [win, off, in1], [out],
+            lambda q, e, T, P: q.tensor_tensor(ap(T, out), ap(T, win).indirect(ap(T, off)), ap(T, in1), op))
 
     def scan(name, out, d0, d1, init, o0, o1):
-        add(name, "ew", out[2] - out[1], "V", [d0, d1] + ([init] if isinstance(init, tuple) else []), [out],
-            lambda q, e, T, P: q.tensor_tensor_scan(ap(T, out), ap(T, d0), ap(T, d1), ap(T, init), o0, o1), io=[d0, d1, out])
+        add(name, "ew", "V", [d0, d1], [out],
+            lambda q, e, T, P: q.tensor_tensor_scan(ap(T, out), ap(T, d0), ap(T, d1), init, o0, o1))
 
     def tt(name, out, in0, in1, op):
-        add(name, "tt", out[2] - out[1], "V", [in0, in1], [out],
+        add(name, "tt", "V", [in0, in1], [out],
             lambda q, e, T, P: q.tensor_tensor(ap(T, out), ap(T, in0), ap(T, in1), op))
 
     def quant(name, cq, cs, a, b, src, a0):
         i = (src, a0, a0 + 4 * (b - a))
-        add(name, "quant", b - a, "V", [i], [(cq, a, b), (cs, a, b)],
+        add(name, "quant", "V", [i], [(cq, a, b), (cs, a, b)],
             lambda q, e, T, P: q.quantize_mx(ap(T, (cq, a, b)), ap(T, (cs, a, b)), ap(T, i)))
 
     def mm(name, tile, lq, ls, l0, rq, rs, a, b, start=True, stop=True, after=()):
         rd = [(lq, l0, l0 + 128), (ls, l0, l0 + 128), (rq, a, b), (rs, a, b)]
-        add(name, "mm", b - a, "T", rd, [("#" + tile, 0, 1)],
-            lambda q, e, T, P: q.matmul_mx(P(tile, b - a), ap(T, rd[0]), ap(T, rd[1]), ap(T, rd[2]), ap(T, rd[3]), start, stop),
+        add(name, "mm", "T", rd, [("#" + tile, 0, 1)],
+            lambda q, e, T, P: q.matmul_mx(P(tile)[:, 0:b - a], ap(T, rd[0]), ap(T, rd[1]), ap(T, rd[2]), ap(T, rd[3]), start, stop),
             tile=tile, start=start, after=list(after))
 
     def evac(name, out, tile, n, scale):
         def em(q, e, T, P):
             if e == "S":
-                return q.activation(ap(T, out), P(tile, n), F.Copy, scale=scale)
-            return q.tensor_scalar(ap(T, out), P(tile, n), scale, None, A.mult)
-        add(name, "ew", n, "SV", [("#" + tile, 0, 1)], [out], em, frees=tile)
+                return q.activation(ap(T, out), P(tile)[:, 0:n], F.Copy, scale=scale)
+            return q.tensor_scalar(ap(T, out), P(tile)[:, 0:n], scale, None, A.mult)
+        add(name, "ew", "SV", [("#" + tile, 0, 1)], [out], em, frees=tile)
 
-    def own(x, a, b):
-        return (x, B0 + a, B0 + b)
+    def hold(name, out, src, table):
+        scan(name, out, src, table, -DROP, A.max, A.add)
 
-    def upto(x, b):
-        return (x, 0, B0 + b)
+    def to_list(name, lst, tmp, scale):
+        ts(name, lst, (tmp[0], tmp[1] + 15, tmp[2], 16), ("corr", 0, 1), scale / UNIT, A.subtract, A.mult)
 
-    def to_list(tag, lst, tmp, src, a, b):
-        scan("cs" + tag, (tmp, a, b), ("dd", a, b), own(src, a, b), 0.0, A.add, A.max)
-        ts("ct" + tag, (lst, a // 16, b // 16), (tmp, a + 15, b, 16), ("corr", 0, 1), 1.0 / UNIT, A.subtract, A.mult)
+    runs_ = cfg["RUNS"]
+    nr = len(runs_)
+    size = [b - a for a, b in runs_]
+    wid = [n // RADIX for n in size]
+    cols = [(w // 16 + 1) // 2 * 2 for w in wid]
+    lv = max(size) + 8
 
-    load("ldd", "YS", ("ds", 0, M), lambda T: T.dist[:, :], 4 * M)
-    load("ldu", "YS", ("us", 0, 512), lambda T: T.u[:, :], 1024)
-    for i, (a, b) in enumerate(cfg["TCH"][0]):
-        load("ldx%d" % i, "YS", ("xs", 4 * a, 4 * b), lambda T, a=a, b=b: T.x[:, 4 * a:4 * b], 8 * (b - a))
-    load("ldw", "Y", ("wq", 0, 512), lambda T: T.wc[:, :], 2048, codes=True)
-    load("lds", "Y", ("wsc", 0, 512), lambda T: T.ws[:, :], 512)
-    load("ldv", "Y", ("vs", 0, 512), lambda T: T.v[:, :], 1024)
+    def data(k, r):
+        return C + lv * ((k - 1) * nr + r) + 1 if k else runs_[r][0]
 
-    iota("ip", ("ip", 0, 1), [[0, 1]], 0, 1)
-    iota("i16", ("i16", 0, M), [[16, M]], 0, 0)
-    iota("t16", ("t16", 0, 16), [[1, 16]], 0, 0, False)
-    iota("pl0", ("pl", 0, B0), [[1, H], [0, 4]], -H, 0, False)
-    iota("pl1", ("pl", B0, WW), [[1, C]], 0, 0, False)
-    fill("cs4", ("cst", 0, H), 2 * UNIT)
-    fill("cs1", ("cst", H, H + C), UNIT / 2)
-    scan("it0", ("it", 0, H), ("cst", 0, H), ("cst", 0, H), -(ZERO + 4) * UNIT, A.add, A.add)
-    scan("it1", ("it", H, H + C), ("cst", H, H + C), ("cst", H, H + C), -(H + 1) * UNIT, A.add, A.add)
+    def part(x, k, r, s):
+        return (x, data(k - 1, r) + s, data(k - 1, r) + size[r], RADIX)
+
+    def slot(x, k, r, s):
+        return (x, data(k, r) + wid[r] * s, data(k, r) + wid[r] * (s + 1))
+
+    def lcol(k, r, s):
+        return 9 * sum(cols[:r]) + cols[r] * (3 * (k - 1) + s - 1)
+
+    def table(x, k, r):
+        return (x, W * (k - 1) + sum(wid[:r]), W * (k - 1) + sum(wid[:r + 1]))
+
+    def level(tag, x, k, r, op):
+        if k > 1 or x == "xb":
+            cp("%sc%d%d" % (tag, k, r), slot(x, k, r, 0), part(x, k, r, 0), "SV")
+        for s in range(1, RADIX):
+            o = lcol(k, r, s)
+            gtt("%s%d%d%d" % (tag, k, s, r), slot(x, k, r, s), (x, data(k, r) - 1, data(k, r) + wid[r] * s),
+                ("ll", o, o + wid[r] // 16), part(x, k, r, s), op)
+
+    def block(x, n):
+        r = [i for i in range(nr) if runs_[i][0] <= BLK * n][-1]
+        return (x, data(LEVELS, r) + n - runs_[r][0] // BLK, data(LEVELS, r) + size[r], size[r] // BLK)
+
+    load("ldd", "S", ("ds", 0, M), lambda T: T.dist[:, :])
+    before = "ldd"
+    for nm in cfg["LORD"]:
+        if nm == "u":
+            load("ldu", "Y", ("us", 0, 512), lambda T: T.u[:, :], after=[before])
+        else:
+            a, b = cfg["XCH"][int(nm[1])]
+            load("ld" + nm, "Y", ("xs", 4 * a, 4 * b), lambda T, a=a, b=b: T.x[:, 4 * a:4 * b], after=[before])
+        before = "ld" + nm
+    load("ldw", "Y", ("wq", 0, 512), lambda T: T.wc[:, :], codes=True, behind=[("xs", 0, 4 * C), ("us", 0, 512)])
+    load("lds", "Y", ("wsc", 0, 512), lambda T: T.ws[:, :], after=["ldw"])
+    load("ldv", "Y", ("vs", 0, 512), lambda T: T.v[:, :], after=["lds"])
+
+    iota("ip", ("ip", 0, 16), [[0, 16]], 0, 1)
+    iota("rr", ("ip", 16, 32), [[1, 16]], 128, -1)
+    iota("i16", ("i16", 0, M), [[16, M]], H, 0, False)
+    fill("cst", ("cst", 0, WW // 2), UNIT / 2)
+    scan("it0", ("it", 0, WW // 2), ("cst", 0, WW // 2), ("cst", 0, WW // 2), -(WW + 1) * UNIT, A.add, A.add)
+    lin("it1", ("it", WW // 2, WW), ("it", 0, WW // 2), 1.0, WW // 2 * UNIT)
+    cp("hrb", ("rb", 0, H), ("it", 0, H), "SV")
+    fill("xd", ("xb", C, C + lv * LEVELS * nr, lv), 1.0)
+    fill("ed", ("eb", C, C + lv * LEVELS * nr, lv), -1.0)
+    for r in range(nr):
+        if 16 * cols[r] > wid[r]:
+            fill("tmd%d" % r, ("tm", 16 * lcol(1, r, 2) - 1, 16 * lcol(LEVELS, r, RADIX), 16 * cols[r]), 0.0)
     fill("g64", ("gsel", 0, 516), 64.0)
-    add("sel", "iota", 516, "G", [("gsel", 0, 516)], [("gsel", 0, 516)],
+    add("sel", "iota", "G", [("gsel", 0, 516)], [("gsel", 0, 516)],
         lambda q, e, T, P: q.affine_select(T.gsel[:, 0:516], T.gsel[:, 0:516], [[1, 516]], A.is_equal, 0.0, -3, -4))
-    ts("pmi", ("pmi", 0, 1), ("ip", 0, 1), 15, None, A.bitwise_and)
-    cp("pm", ("pm", 0, 1), ("pmi", 0, 1))
-    ts("pm1", ("pm1", 0, 1), ("pm", 0, 1), 1.0, None, A.add)
-    ts("cor0", ("corr", 1, 2), ("pm", 0, 1), 15.0, LIFT, A.is_lt, A.mult)
-    ts("corr", ("corr", 0, 1), ("corr", 1, 2), -ZERO * UNIT, None, A.add)
-    ts("jw", ("jw", 0, M), ("i16", 0, M), ("pm", 0, 1), float(H), A.add, A.add)
-    ts("lp", ("lp", 0, M), ("i16", 0, M), 0.0, ("pm", 0, 1), A.mult, A.add)
-    cp("uo", ("uo", 0, 8), ("i16", 0, 8))
-    ts("d0", ("d0", 0, 16), ("t16", 0, 16), ("pm", 0, 1), -2.0, A.is_equal, A.mult)
-    ts("d1", ("d1", 0, 16), ("t16", 0, 16), ("pm1", 0, 1), LIFT, A.is_equal, A.mult)
-    tt("d2", ("d2", 0, 16), ("d0", 0, 16), ("d1", 0, 16), A.add)
-    gather("dd", ("dd", 0, C), ("d2", 0, 16), 0, C, "lp")
-    for x in ("w0", "w1", "w2", "e0", "e1", "e2"):
-        cp("h" + x, (x, 0, B0, 4), ("it", 0, H), "SV")
+    ts("qi", ("qi", 0, 32), ("ip", 0, 32), 15, None, A.bitwise_and)
+    cp("qf", ("qf", 0, 32), ("qi", 0, 32))
+    cp("lp", ("lp", 0, 16), ("qi", 0, 16))
+    lin("jw", ("jw", 0, M), ("i16", 0, M), 1.0, ("qf", 0, 1))
+    ts("uo", ("uo", 0, 8), ("i16", 0, 8), float(H), None, A.subtract)
+    flag("d0", ("d0", 0, 16), ("qf", 16, 32), 0.0, -1.0, 1.0)
+    flag("d1", ("d1", 0, 16), ("qf", 16, 32), 15.0, 1.0, DROP)
+    tt("d2", ("d2", 0, 16), ("d0", 0, 16), ("d1", 0, 16), A.subtract)
+    lin("corr", ("corr", 0, 1), ("d1", 15, 16), -1.0, LIFT - WW * UNIT)
+    gather("cw", ("cw", 0, W), ("d2", 0, 16), ("lp", 0, W // 16))
+    ts("dd", ("dd", 0, BLK), ("cw", 0, BLK), LIFT, None, A.min)
+    for k in range(1, LEVELS + 1):
+        for r in range(nr):
+            R = size[r] // RADIX ** k
+            step, base = (size[r] - 1) / R, LIFT + (1.25 / R - H - runs_[r][0]) * UNIT
+            if k == 1:
+                lin("val1%d" % r, table("val", k, r), ("it", 0, wid[r]), -step, base - step * WW * UNIT)
+            else:
+                iota("nt%d%d" % (k, r), table("nt", k, r), [[0, wid[r] // R], [1, R]], 0, 0, False)
+                lin("val%d%d" % (k, r), table("val", k, r), table("nt", k, r), -step * UNIT, base)
+        scan("dd%d" % k, ("ddk", W * (k - 1), W * k), ("val", W * (k - 1), W * k), ("cw", 0, W), 0.0, A.max, A.min)
     for b in range(4):
         quant("qe%d" % b, "qe", "se", 128 * b, 128 * b + 128, "gsel", 3 - b)
     quant("qu", "qu", "su", 0, 128, "us", 0)
-    add("pu", "gather", 128, "V", [("qu", 0, 128), ("uo", 0, 8)], [("qu2", 0, 128)],
+    add("pu", "gather", "V", [("qu", 0, 128), ("uo", 0, 8)], [("qu2", 0, 128)],
         lambda q, e, T, P: q.tensor_copy(T.qu2[:, 0:128].bitcast(dt.uint32), T.qu[:, 0:128].bitcast(dt.uint32).indirect(T.uo[:, 0:8])))
-    gather("pus", ("su2", 0, 128), ("su", 0, 128), 0, 128, "uo")
+    gather("pus", ("su2", 0, 128), ("su", 0, 128), ("uo", 0, 8))
     quant("qv", "qv", "sv", 0, 128, "vs", 0)
     if first:
         for t in range(ROUNDS):
             for b in range(4):
-                fill("he%d%d" % (t, b), ("f%d" % t, WW * b, WW * b + B0, 4), 0.0)
+                lin("he%d%d" % (t, b), ("f%d" % t, WW * b, WW * b + H), ("cst", 0, H), 0.0, 0.0)
 
     tt("a0", ("a0", 0, M), ("jw", 0, M), ("ds", 0, M), A.subtract)
     cp("ln", ("ln", 0, M), ("a0", 0, M))
-    ts("a1", ("a1", 0, M), ("a0", 0, M), float(H), 3.0, A.min, A.mult)
-    tt("a2", ("a2", 0, M), ("a0", 0, M), ("a1", 0, M), A.add)
-    cp("l0", ("lk0", 0, M), ("a2", 0, M))
-    for k in range(K + 1):
-        for i, (a, b) in enumerate(cfg["LCH"]):
-            if k == K:
-                a = max(a, 1 << K)
-            if k == 0:
-                gather("wg0%d" % i, own("w0", a, b), ("it", 0, H + b), a, b, "ln")
-                if a == 0:
-                    cp("par0", ("par0", 0, 1), own("w0", 0, 1), "SV")
-            else:
-                gather("wg%d%d" % (k, i), own("w%d" % (k % 3), a, b), upto("w%d" % ((k - 1) % 3), b), a, b, "lk%d" % (k - 1))
-                to_list("%d%d" % (k, i), "lk%d" % k, "tm%d" % k, "w%d" % (k % 3), a, b)
+    for i, (a, b) in enumerate(cfg["PCH"]):
+        gather("par%d" % i, ("xb", a, b), ("it", 0, H + b), ("ln", a // 16, b // 16))
+    for r in range(nr):
+        for k in range(1, LEVELS + 1):
+            for s in range(1, RADIX):
+                o = 16 * lcol(k, r, s)
+                hold("xs%d%d%d" % (k, s, r), ("tm", o, o + wid[r]), part("xb", k, r, s), table("ddk", k, r))
+            for a, b in cfg["CT"]:
+                lo, hi = lcol(k, r, a), lcol(k, r, b - 1) + wid[r] // 16
+                to_list("xl%d%d%d" % (k, a, r), ("ll", lo, hi), ("tm", 16 * lo, 16 * hi), size[r] // RADIX ** k)
+            level("x", "xb", k, r, A.min)
+    for n in range(NB):
+        hold("xf%d" % n, ("tf", BLK * n, BLK * n + BLK), block("xb", n), ("dd", 0, BLK))
+    for a, b in cfg["CF"]:
+        to_list("lf%d" % a, ("lf", 4 * a, 4 * b), ("tf", BLK * a, BLK * b), 1.0)
 
-    for i, (a, b) in enumerate(cfg["TCH"][0]):
+    for i, (a, b) in enumerate(cfg["XCH"]):
         quant("qt0%d" % i, "qt0", "st0", a, b, "xs", 4 * a)
     for t in range(ROUNDS):
-        qt, st, ft, ee = "qt%d" % t, "st%d" % t, "f%d" % t, ["e0", "e1", "e2"]
-        halo = [(qt, C - H, C), (st, C - H, C)]
-        if not last:
-            add("snd%d" % t, "send", H, "G", halo, [], None, t=t)
-        if not first:
-            add("arr%d" % t, "arrive", H, "R", halo, [("lq%d" % t, 0, H), ("ls%d" % t, 0, H)], None, t=t,
-                after=[] if last else ["snd%d" % t])
-        for i, (a, b) in enumerate(cfg["TCH"][t]):
+        qt, st, ft = "qt%d" % t, "st%d" % t, "f%d" % t
+        for i, (a, b) in enumerate(cfg["SND"][t]):
+            halo, land = [(qt, a, b), (st, a, b)], [(x % t, a - C + H, b - C + H) for x in ("lq%d", "ls%d")]
+            if not last:
+                add("snd%d%d" % (t, i), "send", "G", halo, [], None, t=t, cut=(a, b), sem="arr%d%d" % (t, i))
+            if not first:
+                add("arr%d%d" % (t, i), "arrive", "R", halo, land, None, t=t, after=[] if last else ["snd%d%d" % (t, i)])
+        for i, (a, b) in enumerate(cfg["PB"][t] or (cfg["TCH"][t - 1] if t else cfg["XCH"])):
             tile = "p%d%d" % (t, i)
             mm("mp%d%d" % (t, i), tile, "qu2", "su2", 0, qt, st, a, b)
-            o = ("sg%d" % t, a, b)
-
-            def em(q, e, T, P, o=o, tile=tile):
-                if e == "S":
-                    return q.activation(ap(T, o), P(tile, o[2] - o[1]), F.Sign, bias=TINY)
-                return q.tensor_scalar(ap(T, o), P(tile, o[2] - o[1]), 0.0, 0.5, A.is_ge, A.subtract)
-            add("sg%d%d" % (t, i), "ew", b - a, "SV", [("#" + tile, 0, 1)], [o], em, frees=tile)
-            scan("fl%d%d" % (t, i), own("e0", max(a, 1), b), ("it", H + max(a, 1), H + b), (o[0], max(a, 1), b), -1.0, A.max, A.min)
-            if a == 0:
-                scan("fx%d" % t, own("e0", 0, 1), (o[0], 0, 1), ("it", H, H + 1), ("par0", 0, 1), A.max, A.min)
+            cuts = [("eb%d%d" % (t, i), a, b, 1, ("eb", a, b))]
+            for r, (c, d) in enumerate(runs_):
+                lo, hi = max(a, c), min(b, d)
+                if lo < hi:
+                    cuts.append(("ea%d%d%d" % (t, i, r), lo, hi, RADIX,
+                                 ("eb", data(1, r) + (lo - c) // RADIX, data(1, r) + (hi - c) // RADIX)))
+            for nm, lo, hi, step, o in cuts:
+                num = ("it", H + lo, H + hi, step)
+                add(nm, "ew", "V", [("#" + tile, 0, 1), num], [o],
+                    lambda q, e, T, P, o=o, num=num, tile=tile, a=a: q.tensor_tensor(
+                        ap(T, o), P(tile)[:, num[1] - H - a:num[2] - H - a:num[3]], ap(T, num), A.min), frees=tile)
         for i, (a, b) in enumerate(cfg["FCH"][t]):
             for p in range(4):
                 tile = "f%d%d%d" % (t, i, p)
                 mm("mf%d%d%d" % (t, i, p), tile, "qe", "se", 128 * p, qt, st, a, b)
-                evac("fe%d%d%d" % (t, i, p), (ft, WW * p + B0 + a, WW * p + B0 + b), tile, b - a, 1.0 / 64)
+                evac("fe%d%d%d" % (t, i, p), (ft, WW * p + H + a, WW * p + H + b), tile, b - a, 1.0 / 64)
         if not first:
             for p in range(4):
                 tile = "h%d%d" % (t, p)
                 mm("mh%d%d" % (t, p), tile, "qe", "se", 128 * p, "lq%d" % t, "ls%d" % t, 0, H)
-                evac("he%d%d" % (t, p), (ft, WW * p, WW * p + B0, 4), tile, H, 1.0 / 64)
-        for k in range(K):
-            for i, (a, b) in enumerate(cfg["VCH"][t]):
-                sh = ("s%d" % (k % 2), a, b)
-                if k == 0:
-                    scan("sh%d0%d" % (t, i), sh, ("it", H + a, H + b), ("sg%d" % t, a, b), -1.0, A.max, A.min)
-                else:
-                    cp("sh%d%d%d" % (t, k, i), sh, own(ee[k % 3], a, b), "SV")
-                gmax("vs%d%d%d" % (t, k, i), own(ee[(k + 1) % 3], a, b), upto(ee[k % 3], b), a, b, "lk%d" % k, sh)
-        B, out, final = 1 << K, ee[K % 3], []
-        for n in range(1, (C - 1) // B + 1):
-            a, b = B * n, min(B * (n + 1), C)
-            gmax("bl%d%d" % (t, n), own(out, a, b), upto(out, a), a, b, "lk%d" % K, own(out, a, b))
-            for i, (a2, b2) in enumerate(cfg["TCH"][t + 1]):
-                if b2 <= b and i not in final:
-                    final.append(i)
-                    to_list("r%d%d" % (t, i), "lr%d" % t, "rt%d" % t, out, a2, b2)
+                evac("he%d%d" % (t, p), (ft, WW * p, WW * p + H), tile, H, 1.0 / 64)
+        for r in range(nr):
+            for k in range(1, LEVELS + 1):
+                level("e%d" % t, "eb", k, r, A.max)
+        runs, chunks = cfg["SB"][t] or [(BLK * n, BLK * n + BLK) for n in range(NB)], cfg["TCH"][t]
+        for n in range(NB):
+            a, b = BLK * n, BLK * n + BLK
+            gtt("bl%d%d" % (t, n), ("rb", H + a, H + b), ("rb", 0, H + a), ("lf", 4 * n, 4 * n + 4), block("eb", n), A.max)
+        for i, (a, b) in enumerate(runs):
+            hold("rs%d%d" % (t, i), ("rt%d" % t, a, b), ("rb", H + a, H + b), ("dd", 0, b - a))
         z, qz, sz, tn = "z%d" % t, "qz%d" % t, "sz%d" % t, "t%d" % (t + 1)
-        for i, (a, b) in enumerate(cfg["TCH"][t + 1]):
-            g = "%d%d" % (t, i)
+        for i, (a, b) in enumerate(cfg["ZB"][t] or chunks):
+            g, lr = "%d%d" % (t, i), ("lr%d" % t, a // 16, b // 16)
+            to_list("rl" + g, lr, ("rt%d" % t, a, b), 1.0)
             for p in range(4):
-                gather("zg%s%d" % (g, p), (z, 4 * a + p, 4 * b, 4), (ft, WW * p, WW * p + B0 + b), a, b, "lr%d" % t)
+                gather("zg%s%d" % (g, p), (z, 4 * a + p, 4 * b, 4), (ft, WW * p, WW * p + H + b), lr)
+        for i, (a, b) in enumerate(chunks):
+            g = "%d%d" % (t, i)
             quant("qz" + g, qz, sz, a, b, z, 4 * a)
             for p in range(4):
-                mm("me%s%d" % (g, p), "s%s%d" % (g, p), "qe", "se", 128 * p, qt, st, a, b, True, False, after=["zg%s0" % g])
+                mm("me%s%d" % (g, p), "s%s%d" % (g, p), "qe", "se", 128 * p, qt, st, a, b, True, False,
+                   after=["he%d%d" % (t, x) for x in range(4)])
             for p in range(4):
                 mm("mw%s%d" % (g, p), "s%s%d" % (g, p), "wq", "wsc", 128 * p, qz, sz, a, b, False, True)
                 evac("te%s%d" % (g, p), (tn, 4 * a + p, 4 * b, 4), "s%s%d" % (g, p), b - a, 1.0 / 64)
             quant("qt%d%d" % (t + 1, i), "qt%d" % (t + 1), "st%d" % (t + 1), a, b, tn, 4 * a)
-    gather("ol", ("olb", 0, C), ("pl", 0, WW), 0, C, "lr%d" % (ROUNDS - 1))
-    store("sol", [("olb", 0, C)], lambda q, e, T, P: q.dma_start(T.ol[:, :], T.olb[0:128:16, :]), 100)
-    for i, (a, b) in enumerate(cfg["TCH"][ROUNDS]):
+    lin("ol", ("olb", 0, C), ("rb", H, WW), 1.0 / UNIT, float(C))
+    store("sol", [("olb", 0, C)], lambda q, e, T, P: q.dma_start(T.ol[:, :], T.olb[0:128:16, :]))
+    for i, (a, b) in enumerate(cfg["TCH"][ROUNDS - 1]):
         mm("my%d" % i, "y%d" % i, "qv", "sv", 0, "qt2", "st2", a, b)
         evac("ye%d" % i, ("yb", a, b), "y%d" % i, b - a, 1.0)
-        store("sy%d" % i, [("yb", a, b)], lambda q, e, T, P, a=a, b=b: q.dma_start(T.y[:, a:b], T.yb[:, a:b]), 4 * (b - a))
+        store("sy%d" % i, [("yb", a, b)], lambda q, e, T, P, a=a, b=b: q.dma_start(T.y[:, a:b], T.yb[:, a:b]))
         store("sc%d" % i, [("qt2", a, b)],
-              lambda q, e, T, P, a=a, b=b: q.dma_start(T.oc[:, 4 * a:4 * b], T.qt2[:, a:b].bitcast(dt.uint8)), 4 * (b - a))
+              lambda q, e, T, P, a=a, b=b: q.dma_start(T.oc[:, 4 * a:4 * b], T.qt2[:, a:b].bitcast(dt.uint8)))
     for k in range(4):
         store("ss%d" % k, [("st2", 0, C)],
-              lambda q, e, T, P, k=k: q.dma_start(T.osc[4 * k:4 * k + 4, :], T.st2[32 * k:32 * k + 4, :]), 100)
+              lambda q, e, T, P, k=k: q.dma_start(T.osc[4 * k:4 * k + 4, :], T.st2[32 * k:32 * k + 4, :]))
 
     for j, o in enumerate(ops):
         o["deps"] = [p["name"] for p in ops[:j]
@@ -334,17 +398,22 @@ def emit(g, core, T, topo, ops, order, prev, nxt):
     seq = [(n, e if e in by[n]["engs"] else by[n]["engs"][0]) for n, e in order if n in by]
     assert sorted(n for n, e in seq) == sorted(by)
     queue = {"V": g.vector, "S": g.scalar, "T": g.tensor, "G": g, "Y": g.sync}
-    free, bank, waits = [(b, None) for b in range(8)], {}, {}
+    readers = {}
+    for o in ops:
+        if "frees" in o:
+            readers.setdefault(o["frees"], []).append(o["name"])
+    free, bank, waits, seen = [(b, []) for b in range(8)], {}, {}, set()
     for n, e in seq:
         o = by[n]
         d = [] if o["kind"] == "arrive" else list(o["deps"])
         if o.get("start"):
             bank[o["tile"]], who = free.pop(0)
-            d += [who] if who else []
+            d += who
         elif o["kind"] == "mm":
             d = [x for x in d if by[x].get("tile") != o["tile"]]
-        if "frees" in o:
-            free.append((bank[o["frees"]], n))
+        seen.add(n)
+        if "frees" in o and seen.issuperset(readers[o["frees"]]):
+            free.append((bank[o["frees"]], readers[o["frees"]]))
         waits[n] = d
     needed = set(x for d in waits.values() for x in d)
     total, done, known = {}, {}, {e: {} for e in queue}
@@ -355,6 +424,7 @@ def emit(g, core, T, topo, ops, order, prev, nxt):
 
     for n, e in seq:
         o = by[n]
+        LABEL[0] = n
         if o["kind"] == "arrive":
             done[n] = (bump(n, 2 * len(topo.engines(prev, core))), {})
             continue
@@ -373,12 +443,13 @@ def emit(g, core, T, topo, ops, order, prev, nxt):
         if o["kind"] == "send":
             rid, pid, _ = topo.addr(nxt)
             t, m = o["t"], topo.mask(core, nxt)
-            g.remote_dma(T["lq%d" % t][:, 0:H].bitcast(dt.uint8), T["qt%d" % t][:, C - H:C].bitcast(dt.uint8),
-                         T.sem["arr%d" % t], T.sem.sent, pid, rid, m)
-            g.remote_dma(T["ls%d" % t][:, 0:H], T["st%d" % t][:, C - H:C], T.sem["arr%d" % t], T.sem.sent, pid, rid, m)
+            a, b = o["cut"]
+            g.remote_dma(T["lq%d" % t][:, a - C + H:b - C + H].bitcast(dt.uint8), T["qt%d" % t][:, a:b].bitcast(dt.uint8),
+                         T.sem[o["sem"]], T.sem.sent, pid, rid, m)
+            g.remote_dma(T["ls%d" % t][:, a - C + H:b - C + H], T["st%d" % t][:, a:b], T.sem[o["sem"]], T.sem.sent, pid, rid, m)
             bump("sent", 2 * len(topo.engines(core, nxt)))
             continue
-        ins = o["em"](q, e, T, lambda tile, w: T["ps%d" % bank[tile]][:, 0:w])
+        ins = o["em"](q, e, T, lambda tile: T["ps%d" % bank[tile]])
         if o["kind"] == "load":
             ins.then_inc(T.sem[n], 16)
             done[n] = (bump(n, 16), dict(kn))

@@ -7,32 +7,33 @@ RADIX, LEVELS = 4, 3
 W = C // RADIX
 BLK = RADIX ** LEVELS
 NB = C // BLK
-CFG = {"RUNS": [(0, 192), (192, 448)], "XCH": [(0, 192), (192, 448)],
-       "TCH": [[(0, 192), (192, 320), (320, 448)], [(0, 192), (192, 320), (320, 448)]],
-       "FCH": [[(0, 448)], [(0, 448)]], "PCH": [(0, 192), (192, 448)], "SND": [[(256, 448)], [(256, 448)]],
-       "CT": [(1, 4)], "CF": [(0, 3), (3, 7)], "SB": [None, None], "ZB": [None, None], "PB": [None, None],
-       "LORD": ["u", "x0", "x1"]}
+A2, A3, A4 = [(0, 192), (192, 448)], [(0, 192), (192, 320), (320, 448)], [(0, 128), (128, 192), (192, 320), (320, 448)]
+CFG = {"RUNS": A2, "XCH": A2, "TCH": [A3, A3], "FCH": [[(0, 448)], [(0, 448)]], "PCH": A2,
+       "SND": [[(256, 448)], [(256, 320), (320, 448)]], "ZB": [A4, A4], "CT": [(1, 4)], "CF": [(1, 3), (3, 4), (4, 7)],
+       "LORD": ["u", "x0", "x1"], "DUP": [[], [0, 1]]}
 ORDER = """
-lddS lduY ldx0Y rrG ipG nt21G i16G xdV cstV tmd0V edV qiV nt30G it0V qfV val10S nt20G g64V jwV d1S d0S nt31G val21S
-hrbS uoV ldx1Y val20S lpV a0V d2V val11V lnV cwV quV dd1V it1S corrS selG par0S ddV puV xs110V xs120V par1S xs130V
-qe2V qt00V xc10S val31S xl110V xs131V xs111V val30S pusS xs121V mp00T dd2V x110V xl111V xc11S dd3V x120V ea000V qt01V
-x130V x111V eb00V xc20S ldwY xs220V xs210V xs230V mp01T x121V e0110V xl210V ea011V x131V snd00G ldsY e0120V x210V
-eb01V x220V e0130V xs211V e0111V x230V xs221V xs231V qe3V e0121V xs320V mf002T arr00R fe002S xc21S ldvY e0c20S xl211V
-xs330V xs310V e0210V e0131V x211V xl310V xc30S e0220V qe1V e0c21S x221V x310V e0230V x231V x320V mf001T e0211V e0c30S
-xc31S xs321V xs331V xs311V x330V e0310V mf003T fe003S e0221V mh01T xl311V xf1V xf2V xf0V e0320V x311V e0231V lf0V
-e0330V x321V mh03T qe0V mh00T bl00V x331V e0c31S e0311V he03S fe001S he01S bl01V he00S mh02T mf000T xf4V xf5V he02S
-e0321V xf3V xf6V bl02V e0331V lf3V rs00V rs01V rs02V bl03V fe000S me013T qvV rl00V bl04V me011T rs03V me010T zg003V
-rs04V bl05V me003T zg000S zg002V me001T zg001S bl06V rs05V rl01V qz00V rs06V me000T me012T me002T mw001T zg011S zg013V
-rl02V zg012V zg010S zg021V te001S mw000T mw002T mw003T qz01V me020T te000S te002S te003S zg023V zg020V mw010T mw011T
-zg022S te010S me021T mw013T qt10V qz02V me022T mw012T me023T mp10T te012V te011S eb10V te013S mw022T te022S ea100V
-mw023T mw020T qt11V te023S mw021T te020S mp11T te021V e1110V qt12V snd10G e1120V eb11V e1130V e1c20S mp12T eb12V
-mf100T ea111V ea121V e1210V mf102T mf103T e1111V e1220V e1121V e1230V e1c30S e1131V arr10R mf101T mh12T e1310V e1c21S
-fe101S fe100S mh10T mh11T e1211V fe103S e1320V e1221V e1330V mh13T fe102S he10S e1231V bl10V e1c31V bl11V e1311V he11S
-he13S he12S me111T bl12V e1321V me100T me102T me101T rs11V rs10V rs12V e1331V rl10V zg100S bl13V zg101V rs13V me121T
-me112T bl14V zg102S zg103V rs14V bl15V rl11V me103T qz10V zg110S zg112S me110T zg113V bl16V zg111V mw100T mw102T
-mw103T rs15V rs16V te100S qz11V te102S olS rl12V zg121S mw101T me113T te103V mw112T te101V mw111T me123T solY zg123S
-te111S zg122V zg120V qt20V mw110T te112V mw113T me120T te110S me122T qz12V my0T mw121T te113S qt21V sc0Y ye0V mw123T
-mw120T te121S te120S mw122T te123V my1T te122V sc1Y sy0Y qt22V ye1S sy1S sc2Y my2T ss3Y ss2S ss0S ss1S ye2S sy2Y
+ipG cstV g64V rrG lgV lddS lduY qiV i16G ldx0Y ldx1Y it0V qfV val10S edV d0V d1V nt20G uoV xdV jwS val11S nt21G nt31G
+it1S tmd0V lpV val20S selV corrS d2V a0V val31S cwS nt30G qe2V lnV val21S par0S qe3V qe0V quV pdx00G dd1V qe1V puV
+xs110V par1S pde10G xs120V xs130V dq11V qt00V pusS dd2V xc10S xl110V mp00T xs121V xs111V xs131V ddV val30S x110V dd3V
+xl111V dq20V ea000V x120V xc11S qt01V x130V eb00V mp01T ldwY x111V ldsY xs220V xs210V xs230V mf003T e0110V x121V
+xl210V xc20S eb01V e0120V x210V ea011V x131V e0130V xc21S x220V e0c20S e0111V xs231V xs221V mf001T xs211V x230V fe003S
+e0121V e0210V xl211V xc30S fe001S xs330V xs320V xs310V e0131V mf002T e0220V xl310V x211V e0c21S e0230V x310V mf000T
+hrbS e0c30S x221V e0211V x320V x231V snd00G e0310V fe002S x330V xc31S xs321V xs331V xs311V arr00R mh01T e0221V e0320V
+mh02T xf1V xl311V xf2V e0231V fe000S e0c31S mh00T he00S e0330V he02S he01S x311V lf1V mh03T dq10V bl00V he03S me000T
+x321V e0311V me003T ldvY bl01V me021T x331V e0321V bl02V xf3V me002T rs00V rs01V e0331V xf4V lf3V xf6V xf5V rs02V
+rl00V bl03V lf4V me012T pdx10G rl01V zg002V bl04V xq11V rs03V zg001S zg013V bl05V rs04V dq21V me022T zg003S zg011V
+zg012S zg000S me001T zg010S bl06V me010T rs05V pde00G rl02V qz00V zg020S rs06V zg023V mw000T zg022S mw003T xq10V
+mw002T rl03V mw001T zg021V te000S zg030V qz01V me011T mw012T te003V te002V zg033V mw010T zg031S me020T me013T mw011T
+mw013T te001S zg032S qt10V te012S me023T qz02V xq20V mp10T mw020T mw021T mw022T te010V qvV mw023T xq21V eb10V te011S
+ea100V te013S te020S qt11V te021S te022V e1110V te023S mp11T lq10V qt12V e1120V mp12T mf102T eb11V lq20V ea111V e1130V
+e1c20S e1d10V lq11V fe102S ea121V eb12V mf100T e1210V e1111V e1220V e1c30S e1121V e1d20V e1230V mf103T e1131V snd10G
+e1c21S e1310V e1d11V mf101T lq21V e1320V e1211V fe103S e1330V fe100S arr10R e1221V snd11G fe101S arr11R mh12T mh13T
+bl10V mh11T e1231V e1d21V mh10T bl11V e1c31S he12S rs10V he13S he11S e1311V bl12V rs11V e1321V rs12V rl10V e1331V
+he10S rl11V me113T zg103S me112T zg102V me111T zg100S bl13V me101T zg101S zg110V zg111S bl14V zg113S me103T zg112V
+rs13V me100T rs14V bl15V me110T qz10V rl12V zg122S me102T zg120S mw103T bl16V mw101T rs15V zg121V mw100T te103S rs16V
+mw102T zg123V rl13V me123T qz11V zg131V mw111T te101S te102V zg132V mw112T mw113T te100S zg130S mw110T qt20V me120T
+me122T te113V sc0Y zg133S qz12V te111S te112S my0T te110S me121T ye0S mw121T mw122T qt21V mw123T te121V te122V te123V
+mw120T my1T sy0Y sc1S te120S ye1S qt22V my2T sy1Y olS sc2S ss1S ss3Y ss0S solS ye2S ss2S sy2Y
 """
 
 Q4, U8, BF, F32, I32, U16 = "float8_e4m3fn_x4", "uint8", "bfloat16", "float32", "int32", "uint16"
@@ -49,8 +50,7 @@ _sb("us vs", 512, BF)
 _sb("ds a0", M, I32)
 _sb("i16 jw", M, F32)
 _sb("ip qi", 32, I32)
-_sb("qf", 32, F32)
-_sb("corr d0 d1 d2", 16, F32)
+_sb("qf corr d0 d1 d2", 16, F32)
 _sb("cw", W, F32)
 _sb("wq qe", 512, Q4)
 _sb("wsc se", 512, U8)
@@ -66,10 +66,10 @@ _sb("cst", WW // 2, BF)
 _sb("it rb", WW, F32)
 _sb("xb eb", 2400, F32)
 _sb("nt val ddk", W * LEVELS, F32)
-_sb("dd", BLK, F32)
+_sb("dd dq tq", BLK, F32)
 _sb("tm", 1600, F32)
 _sb("tf rt0 rt1 olb yb", C, F32)
-_sb("uo", 8, U16)
+_sb("uo lg lq", 8, U16)
 _sb("lp", 16, U16)
 _sb("ll", 100, U16)
 _sb("ln lf lr0 lr1", M, U16)
@@ -82,6 +82,7 @@ SEMAPHORES = ["cV", "cS", "cT", "cG", "arr00", "arr10", "arr01", "arr11", "sent"
 UNIT = 2.0 ** -92
 LIFT = 2048 * UNIT
 DROP = 4096 * UNIT
+ROOM = 256
 LABEL = [None]
 
 
@@ -144,13 +145,6 @@ def plan(first, last, cfg):
             return q.tensor_scalar(ap(T, out), ap(T, in_), scale, ap(T, bias), A.mult, A.add)
         add(name, "ew", "SV", [in_] + ([bias] if isinstance(bias, tuple) else []), [out], em)
 
-    def flag(name, out, in_, end, way, size):
-        def em(q, e, T, P):
-            if e == "S":
-                return q.activation(ap(T, out), ap(T, in_), F.Relu, bias=size * (1.0 - way * end), scale=size * way)
-            return q.tensor_scalar(ap(T, out), ap(T, in_), end, size, A.is_equal, A.mult)
-        add(name, "ew", "SV", [in_], [out], em)
-
     def cp(name, out, in_, engs="V"):
         def em(q, e, T, P):
             if e == "S":
@@ -208,15 +202,24 @@ def plan(first, last, cfg):
     wid = [n // RADIX for n in size]
     cols = [(w // 16 + 1) // 2 * 2 for w in wid]
     lv = max(size) + 8
+    twins = [r for r in range(nr) if any(r in d for d in cfg["DUP"])]
 
     def data(k, r):
-        return C + lv * ((k - 1) * nr + r) + 1 if k else runs_[r][0]
+        return ROOM * nr + lv * ((k - 1) * nr + r) + 1 if k else ROOM * r
 
     def part(x, k, r, s):
         return (x, data(k - 1, r) + s, data(k - 1, r) + size[r], RADIX)
 
+    def spot(x, a, b):
+        r = [i for i in range(nr) if runs_[i][0] <= a][-1]
+        assert b <= runs_[r][1]
+        return (x, data(0, r) + a - runs_[r][0], data(0, r) + b - runs_[r][0])
+
     def slot(x, k, r, s):
         return (x, data(k, r) + wid[r] * s, data(k, r) + wid[r] * (s + 1))
+
+    def tip(x, k, r):
+        return (x, data(k - 1, r) + RADIX - 1, data(k - 1, r) + ROOM, 16)
 
     def lcol(k, r, s):
         return 9 * sum(cols[:r]) + cols[r] * (3 * (k - 1) + s - 1)
@@ -224,13 +227,21 @@ def plan(first, last, cfg):
     def table(x, k, r):
         return (x, W * (k - 1) + sum(wid[:r]), W * (k - 1) + sum(wid[:r + 1]))
 
-    def level(tag, x, k, r, op):
-        if k > 1 or x == "xb":
+    def level(tag, x, k, r, op, twin=False):
+        q4 = wid[r] // RADIX
+        if k > 1 and twin:
+            cp("%sc%d%d" % (tag, k, r), (x, data(k, r), data(k, r) + 3 * q4),
+               (x, data(k - 1, r), data(k - 1, r) + 3 * wid[r], RADIX), "SV")
+        elif k > 1 or x == "xb":
             cp("%sc%d%d" % (tag, k, r), slot(x, k, r, 0), part(x, k, r, 0), "SV")
         for s in range(1, RADIX):
             o = lcol(k, r, s)
             gtt("%s%d%d%d" % (tag, k, s, r), slot(x, k, r, s), (x, data(k, r) - 1, data(k, r) + wid[r] * s),
                 ("ll", o, o + wid[r] // 16), part(x, k, r, s), op)
+        if k < LEVELS and twin:
+            o = 4 * r + 2 * (k - 1)
+            gtt("%sd%d%d" % (tag, k, r), (x, data(k + 1, r) + 3 * q4, data(k + 1, r) + 3 * q4 + 16),
+                (x, data(k, r) - 1, data(k, r) + wid[r] * 3), ("lq", o, o + 1), tip(x, k, r), op)
 
     def block(x, n):
         r = [i for i in range(nr) if runs_[i][0] <= BLK * n][-1]
@@ -256,21 +267,27 @@ def plan(first, last, cfg):
     scan("it0", ("it", 0, WW // 2), ("cst", 0, WW // 2), ("cst", 0, WW // 2), -(WW + 1) * UNIT, A.add, A.add)
     lin("it1", ("it", WW // 2, WW), ("it", 0, WW // 2), 1.0, WW // 2 * UNIT)
     cp("hrb", ("rb", 0, H), ("it", 0, H), "SV")
-    fill("xd", ("xb", C, C + lv * LEVELS * nr, lv), 1.0)
-    fill("ed", ("eb", C, C + lv * LEVELS * nr, lv), -1.0)
+    fill("xd", ("xb", ROOM * nr, ROOM * nr + lv * LEVELS * nr, lv), 1.0)
+    fill("ed", ("eb", ROOM * nr, ROOM * nr + lv * LEVELS * nr, lv), -1.0)
+    for r in twins:
+        for k in range(LEVELS - 1):
+            for x in ("xb", "eb"):
+                if size[r] < ROOM:
+                    iota("pd%s%d%d" % (x[0], k, r), (x, data(k, r) + size[r], data(k, r) + ROOM), [[0, ROOM - size[r]]], -1, 0, False)
     for r in range(nr):
         if 16 * cols[r] > wid[r]:
             fill("tmd%d" % r, ("tm", 16 * lcol(1, r, 2) - 1, 16 * lcol(LEVELS, r, RADIX), 16 * cols[r]), 0.0)
-    fill("g64", ("gsel", 0, 516), 64.0)
-    add("sel", "iota", "G", [("gsel", 0, 516)], [("gsel", 0, 516)],
-        lambda q, e, T, P: q.affine_select(T.gsel[:, 0:516], T.gsel[:, 0:516], [[1, 516]], A.is_equal, 0.0, -3, -4))
     ts("qi", ("qi", 0, 32), ("ip", 0, 32), 15, None, A.bitwise_and)
-    cp("qf", ("qf", 0, 32), ("qi", 0, 32))
+    cp("qf", ("qf", 0, 1), ("qi", 0, 1))
     cp("lp", ("lp", 0, 16), ("qi", 0, 16))
     lin("jw", ("jw", 0, M), ("i16", 0, M), 1.0, ("qf", 0, 1))
     ts("uo", ("uo", 0, 8), ("i16", 0, 8), float(H), None, A.subtract)
-    flag("d0", ("d0", 0, 16), ("qf", 16, 32), 0.0, -1.0, 1.0)
-    flag("d1", ("d1", 0, 16), ("qf", 16, 32), 15.0, 1.0, DROP)
+    ts("d0", ("d0", 0, 16), ("qi", 16, 32), 0.0, 64.0, A.is_equal, A.mult)
+    fill("g64", ("gsel", 0, 516), 0.0)
+    ts("lg", ("lg", 0, 1), ("ip", 0, 1), 4.0, 3.0, A.mult, A.add)
+    add("sel", "gather", "V", [("d0", 0, 16), ("lg", 0, 1)], [("gsel", 0, 516)],
+        lambda q, e, T, P: q.tensor_copy(T.gsel[:, 0:516].indirect(T.lg[:, 0:1]), T.d0[:, 0:16]))
+    ts("d1", ("d1", 0, 16), ("qi", 16, 32), 15.0, DROP, A.is_equal, A.mult)
     tt("d2", ("d2", 0, 16), ("d0", 0, 16), ("d1", 0, 16), A.subtract)
     lin("corr", ("corr", 0, 1), ("d1", 15, 16), -1.0, LIFT - WW * UNIT)
     gather("cw", ("cw", 0, W), ("d2", 0, 16), ("lp", 0, W // 16))
@@ -300,7 +317,7 @@ def plan(first, last, cfg):
     tt("a0", ("a0", 0, M), ("jw", 0, M), ("ds", 0, M), A.subtract)
     cp("ln", ("ln", 0, M), ("a0", 0, M))
     for i, (a, b) in enumerate(cfg["PCH"]):
-        gather("par%d" % i, ("xb", a, b), ("it", 0, H + b), ("ln", a // 16, b // 16))
+        gather("par%d" % i, spot("xb", a, b), ("it", 0, H + b), ("ln", a // 16, b // 16))
     for r in range(nr):
         for k in range(1, LEVELS + 1):
             for s in range(1, RADIX):
@@ -309,8 +326,14 @@ def plan(first, last, cfg):
             for a, b in cfg["CT"]:
                 lo, hi = lcol(k, r, a), lcol(k, r, b - 1) + wid[r] // 16
                 to_list("xl%d%d%d" % (k, a, r), ("ll", lo, hi), ("tm", 16 * lo, 16 * hi), size[r] // RADIX ** k)
+            if k < LEVELS and r in twins:
+                o, v = 4 * r + 2 * (k - 1), table("val", k, r)
+                dq, tq = ("dq", 8 * o, 8 * o + 16), ("tq", 8 * o, 8 * o + 16)
+                scan("dq%d%d" % (k, r), dq, (v[0], v[1], v[1] + 64, RADIX), ("cw", 0, 16), 0.0, A.max, A.min)
+                hold("xq%d%d" % (k, r), tq, tip("xb", k, r), dq)
+                to_list("lq%d%d" % (k, r), ("lq", o, o + 1), tq, size[r] // RADIX ** k)
             level("x", "xb", k, r, A.min)
-    for n in range(NB):
+    for n in range(1, NB):
         hold("xf%d" % n, ("tf", BLK * n, BLK * n + BLK), block("xb", n), ("dd", 0, BLK))
     for a, b in cfg["CF"]:
         to_list("lf%d" % a, ("lf", 4 * a, 4 * b), ("tf", BLK * a, BLK * b), 1.0)
@@ -325,10 +348,10 @@ def plan(first, last, cfg):
                 add("snd%d%d" % (t, i), "send", "G", halo, [], None, t=t, cut=(a, b), sem="arr%d%d" % (t, i))
             if not first:
                 add("arr%d%d" % (t, i), "arrive", "R", halo, land, None, t=t, after=[] if last else ["snd%d%d" % (t, i)])
-        for i, (a, b) in enumerate(cfg["PB"][t] or (cfg["TCH"][t - 1] if t else cfg["XCH"])):
+        for i, (a, b) in enumerate(cfg["TCH"][t - 1] if t else cfg["XCH"]):
             tile = "p%d%d" % (t, i)
             mm("mp%d%d" % (t, i), tile, "qu2", "su2", 0, qt, st, a, b)
-            cuts = [("eb%d%d" % (t, i), a, b, 1, ("eb", a, b))]
+            cuts = [("eb%d%d" % (t, i), a, b, 1, spot("eb", a, b))]
             for r, (c, d) in enumerate(runs_):
                 lo, hi = max(a, c), min(b, d)
                 if lo < hi:
@@ -351,20 +374,21 @@ def plan(first, last, cfg):
                 evac("he%d%d" % (t, p), (ft, WW * p, WW * p + H), tile, H, 1.0 / 64)
         for r in range(nr):
             for k in range(1, LEVELS + 1):
-                level("e%d" % t, "eb", k, r, A.max)
-        runs, chunks = cfg["SB"][t] or [(BLK * n, BLK * n + BLK) for n in range(NB)], cfg["TCH"][t]
-        for n in range(NB):
+                level("e%d" % t, "eb", k, r, A.max, r in cfg["DUP"][t])
+        tt("bl%d0" % t, ("rb", H, H + BLK), block("xb", 0), block("eb", 0), A.max)
+        for n in range(1, NB):
             a, b = BLK * n, BLK * n + BLK
             gtt("bl%d%d" % (t, n), ("rb", H + a, H + b), ("rb", 0, H + a), ("lf", 4 * n, 4 * n + 4), block("eb", n), A.max)
-        for i, (a, b) in enumerate(runs):
-            hold("rs%d%d" % (t, i), ("rt%d" % t, a, b), ("rb", H + a, H + b), ("dd", 0, b - a))
+        for n in range(NB):
+            a, b = BLK * n, BLK * n + BLK
+            hold("rs%d%d" % (t, n), ("rt%d" % t, a, b), ("rb", H + a, H + b), ("dd", 0, BLK))
         z, qz, sz, tn = "z%d" % t, "qz%d" % t, "sz%d" % t, "t%d" % (t + 1)
-        for i, (a, b) in enumerate(cfg["ZB"][t] or chunks):
+        for i, (a, b) in enumerate(cfg["ZB"][t]):
             g, lr = "%d%d" % (t, i), ("lr%d" % t, a // 16, b // 16)
             to_list("rl" + g, lr, ("rt%d" % t, a, b), 1.0)
             for p in range(4):
                 gather("zg%s%d" % (g, p), (z, 4 * a + p, 4 * b, 4), (ft, WW * p, WW * p + H + b), lr)
-        for i, (a, b) in enumerate(chunks):
+        for i, (a, b) in enumerate(cfg["TCH"][t]):
             g = "%d%d" % (t, i)
             quant("qz" + g, qz, sz, a, b, z, 4 * a)
             for p in range(4):

from concourse.mybir import dt, AluOpType, ActivationFunctionType

C, H, ROUNDS = 448, 192, 2
M = C // 16
WW = H + C
RADIX, LEVELS = 4, 3
W = C // RADIX
BLK = RADIX ** LEVELS
NB = C // BLK
A2, A3, A4 = [(0, 192), (192, 448)], [(0, 192), (192, 320), (320, 448)], [(0, 128), (128, 192), (192, 320), (320, 448)]
CFG = {"RUNS": A2, "XCH": A2, "TCH": [A3, A3], "FCH": [[(0, 448)], [(0, 448)]], "PCH": A2,
       "SND": [[(256, 448)], [(256, 320), (320, 448)]], "ZB": [A4, A4], "CT": [(1, 4)], "CF": [(1, 3), (3, 4), (4, 7)],
       "LORD": ["u", "x0", "x1"], "DUP": [[], [0, 1]]}
ORDER = """
ipG cstV g64V rrG lgV lddS lduY qiV i16G ldx0Y ldx1Y it0V qfV val10S edV d0V d1V nt20G uoV xdV jwS val11S nt21G nt31G
it1S tmd0V lpV val20S selV corrS d2V a0V val31S cwS nt30G qe2V lnV val21S par0S qe3V qe0V quV pdx00G dd1V qe1V puV
xs110V par1S pde10G xs120V xs130V dq11V qt00V pusS dd2V xc10S xl110V mp00T xs121V xs111V xs131V ddV val30S x110V dd3V
xl111V dq20V ea000V x120V xc11S qt01V x130V eb00V mp01T ldwY x111V ldsY xs220V xs210V xs230V mf003T e0110V x121V
xl210V xc20S eb01V e0120V x210V ea011V x131V e0130V xc21S x220V e0c20S e0111V xs231V xs221V mf001T xs211V x230V fe003S
e0121V e0210V xl211V xc30S fe001S xs330V xs320V xs310V e0131V mf002T e0220V xl310V x211V e0c21S e0230V x310V mf000T
hrbS e0c30S x221V e0211V x320V x231V snd00G e0310V fe002S x330V xc31S xs321V xs331V xs311V arr00R mh01T e0221V e0320V
mh02T xf1V xl311V xf2V e0231V fe000S e0c31S mh00T he00S e0330V he02S he01S x311V lf1V mh03T dq10V bl00V he03S me000T
x321V e0311V me003T ldvY bl01V me021T x331V e0321V bl02V xf3V me002T rs00V rs01V e0331V xf4V lf3V xf6V xf5V rs02V
rl00V bl03V lf4V me012T pdx10G rl01V zg002V bl04V xq11V rs03V zg001S zg013V bl05V rs04V dq21V me022T zg003S zg011V
zg012S zg000S me001T zg010S bl06V me010T rs05V pde00G rl02V qz00V zg020S rs06V zg023V mw000T zg022S mw003T xq10V
mw002T rl03V mw001T zg021V te000S zg030V qz01V me011T mw012T te003V te002V zg033V mw010T zg031S me020T me013T mw011T
mw013T te001S zg032S qt10V te012S me023T qz02V xq20V mp10T mw020T mw021T mw022T te010V qvV mw023T xq21V eb10V te011S
ea100V te013S te020S qt11V te021S te022V e1110V te023S mp11T lq10V qt12V e1120V mp12T mf102T eb11V lq20V ea111V e1130V
e1c20S e1d10V lq11V fe102S ea121V eb12V mf100T e1210V e1111V e1220V e1c30S e1121V e1d20V e1230V mf103T e1131V snd10G
e1c21S e1310V e1d11V mf101T lq21V e1320V e1211V fe103S e1330V fe100S arr10R e1221V snd11G fe101S arr11R mh12T mh13T
bl10V mh11T e1231V e1d21V mh10T bl11V e1c31S he12S rs10V he13S he11S e1311V bl12V rs11V e1321V rs12V rl10V e1331V
he10S rl11V me113T zg103S me112T zg102V me111T zg100S bl13V me101T zg101S zg110V zg111S bl14V zg113S me103T zg112V
rs13V me100T rs14V bl15V me110T qz10V rl12V zg122S me102T zg120S mw103T bl16V mw101T rs15V zg121V mw100T te103S rs16V
mw102T zg123V rl13V me123T qz11V zg131V mw111T te101S te102V zg132V mw112T mw113T te100S zg130S mw110T qt20V me120T
me122T te113V sc0Y zg133S qz12V te111S te112S my0T te110S me121T ye0S mw121T mw122T qt21V mw123T te121V te122V te123V
mw120T my1T sy0Y sc1S te120S ye1S qt22V my2T sy1Y olS sc2S ss1S ss3Y ss0S solS ye2S ss2S sy2Y
"""

Q4, U8, BF, F32, I32, U16 = "float8_e4m3fn_x4", "uint8", "bfloat16", "float32", "int32", "uint16"
SCRATCH = {}


def _sb(names, n, d):
    for x in names.split():
        SCRATCH[x] = ("sbuf", [128, n], d)


_sb("xs z0 z1 t1 t2", 4 * C, BF)
_sb("us vs", 512, BF)
_sb("ds a0", M, I32)
_sb("i16 jw", M, F32)
_sb("ip qi", 32, I32)
_sb("qf corr d0 d1 d2", 16, F32)
_sb("cw", W, F32)
_sb("wq qe", 512, Q4)
_sb("wsc se", 512, U8)
_sb("qu qu2 qv", 128, Q4)
_sb("su su2 sv", 128, U8)
_sb("gsel", 520, BF)
_sb("qt0 qt1 qt2 qz0 qz1", C, Q4)
_sb("st0 st1 st2 sz0 sz1", C, U8)
_sb("lq0 lq1", H, Q4)
_sb("ls0 ls1", H, U8)
_sb("f0 f1", 4 * WW, BF)
_sb("cst", WW // 2, BF)
_sb("it rb", WW, F32)
_sb("xb eb", 2400, F32)
_sb("nt val ddk", W * LEVELS, F32)
_sb("dd dq tq", BLK, F32)
_sb("tm", 1600, F32)
_sb("tf rt0 rt1 olb yb", C, F32)
_sb("uo lg lq", 8, U16)
_sb("lp", 16, U16)
_sb("ll", 100, U16)
_sb("ln lf lr0 lr1", M, U16)
for _b in range(8):
    SCRATCH["ps%d" % _b] = ("psum", [128, 512], F32)

LOADS = ["ldd", "ldu", "ldv", "ldw", "lds", "ldx0", "ldx1", "ldx2"]
SEMAPHORES = ["cV", "cS", "cT", "cG", "arr00", "arr10", "arr01", "arr11", "sent", "outY", "outS"] + LOADS

UNIT = 2.0 ** -92
LIFT = 2048 * UNIT
DROP = 4096 * UNIT
ROOM = 256
LABEL = [None]


def _cells(a):
    return range(a[1], a[2], a[3] if len(a) > 3 else 1)


def _meet(a, b):
    if a[0] != b[0] or a[2] <= b[1] or b[2] <= a[1]:
        return False
    if len(a) < 4 and len(b) < 4:
        return True
    return not set(_cells(a)).isdisjoint(_cells(b))


def plan(first, last, cfg):
    A, F = AluOpType, ActivationFunctionType
    ops = []

    def ap(T, a):
        if not isinstance(a, tuple):
            return a
        return T[a[0]][:, a[1]:a[2]:a[3]] if len(a) > 3 else T[a[0]][:, a[1]:a[2]]

    def add(name, kind, engs, reads, writes, em, **kw):
        o = {"name": name, "kind": kind, "engs": engs, "r": reads, "w": writes, "em": em, "after": []}
        o.update(kw)
        ops.append(o)

    def load(name, engs, out, src, codes=False, behind=(), after=()):
        def em(q, e, T, P):
            d = ap(T, out)
            return q.dma_start(d.bitcast(dt.uint8) if codes else d, src(T))
        add(name, "load", engs, list(behind), [out], em, after=list(after))

    def store(name, reads, em):
        add(name, "store", "YS", reads, [], em)

    def iota(name, out, pattern, base, cm, whole=True):
        def em(q, e, T, P):
            if whole:
                return q.iota(ap(T, out), pattern, base, cm)
            return q.iota(ap(T, out), pattern, base, cm, allow_small_or_imprecise_dtypes=True)
        add(name, "iota", "G", [], [out], em)

    def fill(name, out, c):
        add(name, "fill", "V", [], [out], lambda q, e, T, P: q.memset(ap(T, out), c))

    def ts(name, out, in0, s1, s2, o0, o1=None):
        def em(q, e, T, P):
            if o1 is None:
                return q.tensor_scalar(ap(T, out), ap(T, in0), ap(T, s1), None, o0)
            return q.tensor_scalar(ap(T, out), ap(T, in0), ap(T, s1), ap(T, s2), o0, o1)
        add(name, "ew", "V", [in0] + [s for s in (s1, s2) if isinstance(s, tuple)], [out], em)

    def lin(name, out, in_, scale, bias):
        def em(q, e, T, P):
            if e == "S":
                return q.activation(ap(T, out), ap(T, in_), F.Identity, bias=ap(T, bias), scale=scale)
            return q.tensor_scalar(ap(T, out), ap(T, in_), scale, ap(T, bias), A.mult, A.add)
        add(name, "ew", "SV", [in_] + ([bias] if isinstance(bias, tuple) else []), [out], em)

    def cp(name, out, in_, engs="V"):
        def em(q, e, T, P):
            if e == "S":
                return q.activation(ap(T, out), ap(T, in_), F.Copy)
            return q.tensor_copy(ap(T, out), ap(T, in_))
        add(name, "ew", engs, [in_], [out], em)

    def gather(name, out, win, off):
        def em(q, e, T, P):
            s = ap(T, win).indirect(ap(T, off))
            if e == "S":
                return q.activation(ap(T, out), s, F.Copy)
            return q.tensor_copy(ap(T, out), s)
        add(name, "gather", "SV", [win, off], [out], em)

    def gtt(name, out, win, off, in1, op):
        add(name, "gather", "V", [win, off, in1], [out],
            lambda q, e, T, P: q.tensor_tensor(ap(T, out), ap(T, win).indirect(ap(T, off)), ap(T, in1), op))

    def scan(name, out, d0, d1, init, o0, o1):
        add(name, "ew", "V", [d0, d1], [out],
            lambda q, e, T, P: q.tensor_tensor_scan(ap(T, out), ap(T, d0), ap(T, d1), init, o0, o1))

    def tt(name, out, in0, in1, op):
        add(name, "tt", "V", [in0, in1], [out],
            lambda q, e, T, P: q.tensor_tensor(ap(T, out), ap(T, in0), ap(T, in1), op))

    def quant(name, cq, cs, a, b, src, a0):
        i = (src, a0, a0 + 4 * (b - a))
        add(name, "quant", "V", [i], [(cq, a, b), (cs, a, b)],
            lambda q, e, T, P: q.quantize_mx(ap(T, (cq, a, b)), ap(T, (cs, a, b)), ap(T, i)))

    def mm(name, tile, lq, ls, l0, rq, rs, a, b, start=True, stop=True, after=()):
        rd = [(lq, l0, l0 + 128), (ls, l0, l0 + 128), (rq, a, b), (rs, a, b)]
        add(name, "mm", "T", rd, [("#" + tile, 0, 1)],
            lambda q, e, T, P: q.matmul_mx(P(tile)[:, 0:b - a], ap(T, rd[0]), ap(T, rd[1]), ap(T, rd[2]), ap(T, rd[3]), start, stop),
            tile=tile, start=start, after=list(after))

    def evac(name, out, tile, n, scale):
        def em(q, e, T, P):
            if e == "S":
                return q.activation(ap(T, out), P(tile)[:, 0:n], F.Copy, scale=scale)
            return q.tensor_scalar(ap(T, out), P(tile)[:, 0:n], scale, None, A.mult)
        add(name, "ew", "SV", [("#" + tile, 0, 1)], [out], em, frees=tile)

    def hold(name, out, src, table):
        scan(name, out, src, table, -DROP, A.max, A.add)

    def to_list(name, lst, tmp, scale):
        ts(name, lst, (tmp[0], tmp[1] + 15, tmp[2], 16), ("corr", 0, 1), scale / UNIT, A.subtract, A.mult)

    runs_ = cfg["RUNS"]
    nr = len(runs_)
    size = [b - a for a, b in runs_]
    wid = [n // RADIX for n in size]
    cols = [(w // 16 + 1) // 2 * 2 for w in wid]
    lv = max(size) + 8
    twins = [r for r in range(nr) if any(r in d for d in cfg["DUP"])]

    def data(k, r):
        return ROOM * nr + lv * ((k - 1) * nr + r) + 1 if k else ROOM * r

    def part(x, k, r, s):
        return (x, data(k - 1, r) + s, data(k - 1, r) + size[r], RADIX)

    def spot(x, a, b):
        r = [i for i in range(nr) if runs_[i][0] <= a][-1]
        assert b <= runs_[r][1]
        return (x, data(0, r) + a - runs_[r][0], data(0, r) + b - runs_[r][0])

    def slot(x, k, r, s):
        return (x, data(k, r) + wid[r] * s, data(k, r) + wid[r] * (s + 1))

    def tip(x, k, r):
        return (x, data(k - 1, r) + RADIX - 1, data(k - 1, r) + ROOM, 16)

    def lcol(k, r, s):
        return 9 * sum(cols[:r]) + cols[r] * (3 * (k - 1) + s - 1)

    def table(x, k, r):
        return (x, W * (k - 1) + sum(wid[:r]), W * (k - 1) + sum(wid[:r + 1]))

    def level(tag, x, k, r, op, twin=False):
        q4 = wid[r] // RADIX
        if k > 1 and twin:
            cp("%sc%d%d" % (tag, k, r), (x, data(k, r), data(k, r) + 3 * q4),
               (x, data(k - 1, r), data(k - 1, r) + 3 * wid[r], RADIX), "SV")
        elif k > 1 or x == "xb":
            cp("%sc%d%d" % (tag, k, r), slot(x, k, r, 0), part(x, k, r, 0), "SV")
        for s in range(1, RADIX):
            o = lcol(k, r, s)
            gtt("%s%d%d%d" % (tag, k, s, r), slot(x, k, r, s), (x, data(k, r) - 1, data(k, r) + wid[r] * s),
                ("ll", o, o + wid[r] // 16), part(x, k, r, s), op)
        if k < LEVELS and twin:
            o = 4 * r + 2 * (k - 1)
            gtt("%sd%d%d" % (tag, k, r), (x, data(k + 1, r) + 3 * q4, data(k + 1, r) + 3 * q4 + 16),
                (x, data(k, r) - 1, data(k, r) + wid[r] * 3), ("lq", o, o + 1), tip(x, k, r), op)

    def block(x, n):
        r = [i for i in range(nr) if runs_[i][0] <= BLK * n][-1]
        return (x, data(LEVELS, r) + n - runs_[r][0] // BLK, data(LEVELS, r) + size[r], size[r] // BLK)

    load("ldd", "S", ("ds", 0, M), lambda T: T.dist[:, :])
    before = "ldd"
    for nm in cfg["LORD"]:
        if nm == "u":
            load("ldu", "Y", ("us", 0, 512), lambda T: T.u[:, :], after=[before])
        else:
            a, b = cfg["XCH"][int(nm[1])]
            load("ld" + nm, "Y", ("xs", 4 * a, 4 * b), lambda T, a=a, b=b: T.x[:, 4 * a:4 * b], after=[before])
        before = "ld" + nm
    load("ldw", "Y", ("wq", 0, 512), lambda T: T.wc[:, :], codes=True, behind=[("xs", 0, 4 * C), ("us", 0, 512)])
    load("lds", "Y", ("wsc", 0, 512), lambda T: T.ws[:, :], after=["ldw"])
    load("ldv", "Y", ("vs", 0, 512), lambda T: T.v[:, :], after=["lds"])

    iota("ip", ("ip", 0, 16), [[0, 16]], 0, 1)
    iota("rr", ("ip", 16, 32), [[1, 16]], 128, -1)
    iota("i16", ("i16", 0, M), [[16, M]], H, 0, False)
    fill("cst", ("cst", 0, WW // 2), UNIT / 2)
    scan("it0", ("it", 0, WW // 2), ("cst", 0, WW // 2), ("cst", 0, WW // 2), -(WW + 1) * UNIT, A.add, A.add)
    lin("it1", ("it", WW // 2, WW), ("it", 0, WW // 2), 1.0, WW // 2 * UNIT)
    cp("hrb", ("rb", 0, H), ("it", 0, H), "SV")
    fill("xd", ("xb", ROOM * nr, ROOM * nr + lv * LEVELS * nr, lv), 1.0)
    fill("ed", ("eb", ROOM * nr, ROOM * nr + lv * LEVELS * nr, lv), -1.0)
    for r in twins:
        for k in range(LEVELS - 1):
            for x in ("xb", "eb"):
                if size[r] < ROOM:
                    iota("pd%s%d%d" % (x[0], k, r), (x, data(k, r) + size[r], data(k, r) + ROOM), [[0, ROOM - size[r]]], -1, 0, False)
    for r in range(nr):
        if 16 * cols[r] > wid[r]:
            fill("tmd%d" % r, ("tm", 16 * lcol(1, r, 2) - 1, 16 * lcol(LEVELS, r, RADIX), 16 * cols[r]), 0.0)
    ts("qi", ("qi", 0, 32), ("ip", 0, 32), 15, None, A.bitwise_and)
    cp("qf", ("qf", 0, 1), ("qi", 0, 1))
    cp("lp", ("lp", 0, 16), ("qi", 0, 16))
    lin("jw", ("jw", 0, M), ("i16", 0, M), 1.0, ("qf", 0, 1))
    ts("uo", ("uo", 0, 8), ("i16", 0, 8), float(H), None, A.subtract)
    ts("d0", ("d0", 0, 16), ("qi", 16, 32), 0.0, 64.0, A.is_equal, A.mult)
    fill("g64", ("gsel", 0, 516), 0.0)
    ts("lg", ("lg", 0, 1), ("ip", 0, 1), 4.0, 3.0, A.mult, A.add)
    add("sel", "gather", "V", [("d0", 0, 16), ("lg", 0, 1)], [("gsel", 0, 516)],
        lambda q, e, T, P: q.tensor_copy(T.gsel[:, 0:516].indirect(T.lg[:, 0:1]), T.d0[:, 0:16]))
    ts("d1", ("d1", 0, 16), ("qi", 16, 32), 15.0, DROP, A.is_equal, A.mult)
    tt("d2", ("d2", 0, 16), ("d0", 0, 16), ("d1", 0, 16), A.subtract)
    lin("corr", ("corr", 0, 1), ("d1", 15, 16), -1.0, LIFT - WW * UNIT)
    gather("cw", ("cw", 0, W), ("d2", 0, 16), ("lp", 0, W // 16))
    ts("dd", ("dd", 0, BLK), ("cw", 0, BLK), LIFT, None, A.min)
    for k in range(1, LEVELS + 1):
        for r in range(nr):
            R = size[r] // RADIX ** k
            step, base = (size[r] - 1) / R, LIFT + (1.25 / R - H - runs_[r][0]) * UNIT
            if k == 1:
                lin("val1%d" % r, table("val", k, r), ("it", 0, wid[r]), -step, base - step * WW * UNIT)
            else:
                iota("nt%d%d" % (k, r), table("nt", k, r), [[0, wid[r] // R], [1, R]], 0, 0, False)
                lin("val%d%d" % (k, r), table("val", k, r), table("nt", k, r), -step * UNIT, base)
        scan("dd%d" % k, ("ddk", W * (k - 1), W * k), ("val", W * (k - 1), W * k), ("cw", 0, W), 0.0, A.max, A.min)
    for b in range(4):
        quant("qe%d" % b, "qe", "se", 128 * b, 128 * b + 128, "gsel", 3 - b)
    quant("qu", "qu", "su", 0, 128, "us", 0)
    add("pu", "gather", "V", [("qu", 0, 128), ("uo", 0, 8)], [("qu2", 0, 128)],
        lambda q, e, T, P: q.tensor_copy(T.qu2[:, 0:128].bitcast(dt.uint32), T.qu[:, 0:128].bitcast(dt.uint32).indirect(T.uo[:, 0:8])))
    gather("pus", ("su2", 0, 128), ("su", 0, 128), ("uo", 0, 8))
    quant("qv", "qv", "sv", 0, 128, "vs", 0)
    if first:
        for t in range(ROUNDS):
            for b in range(4):
                lin("he%d%d" % (t, b), ("f%d" % t, WW * b, WW * b + H), ("cst", 0, H), 0.0, 0.0)

    tt("a0", ("a0", 0, M), ("jw", 0, M), ("ds", 0, M), A.subtract)
    cp("ln", ("ln", 0, M), ("a0", 0, M))
    for i, (a, b) in enumerate(cfg["PCH"]):
        gather("par%d" % i, spot("xb", a, b), ("it", 0, H + b), ("ln", a // 16, b // 16))
    for r in range(nr):
        for k in range(1, LEVELS + 1):
            for s in range(1, RADIX):
                o = 16 * lcol(k, r, s)
                hold("xs%d%d%d" % (k, s, r), ("tm", o, o + wid[r]), part("xb", k, r, s), table("ddk", k, r))
            for a, b in cfg["CT"]:
                lo, hi = lcol(k, r, a), lcol(k, r, b - 1) + wid[r] // 16
                to_list("xl%d%d%d" % (k, a, r), ("ll", lo, hi), ("tm", 16 * lo, 16 * hi), size[r] // RADIX ** k)
            if k < LEVELS and r in twins:
                o, v = 4 * r + 2 * (k - 1), table("val", k, r)
                dq, tq = ("dq", 8 * o, 8 * o + 16), ("tq", 8 * o, 8 * o + 16)
                scan("dq%d%d" % (k, r), dq, (v[0], v[1], v[1] + 64, RADIX), ("cw", 0, 16), 0.0, A.max, A.min)
                hold("xq%d%d" % (k, r), tq, tip("xb", k, r), dq)
                to_list("lq%d%d" % (k, r), ("lq", o, o + 1), tq, size[r] // RADIX ** k)
            level("x", "xb", k, r, A.min)
    for n in range(1, NB):
        hold("xf%d" % n, ("tf", BLK * n, BLK * n + BLK), block("xb", n), ("dd", 0, BLK))
    for a, b in cfg["CF"]:
        to_list("lf%d" % a, ("lf", 4 * a, 4 * b), ("tf", BLK * a, BLK * b), 1.0)

    for i, (a, b) in enumerate(cfg["XCH"]):
        quant("qt0%d" % i, "qt0", "st0", a, b, "xs", 4 * a)
    for t in range(ROUNDS):
        qt, st, ft = "qt%d" % t, "st%d" % t, "f%d" % t
        for i, (a, b) in enumerate(cfg["SND"][t]):
            halo, land = [(qt, a, b), (st, a, b)], [(x % t, a - C + H, b - C + H) for x in ("lq%d", "ls%d")]
            if not last:
                add("snd%d%d" % (t, i), "send", "G", halo, [], None, t=t, cut=(a, b), sem="arr%d%d" % (t, i))
            if not first:
                add("arr%d%d" % (t, i), "arrive", "R", halo, land, None, t=t, after=[] if last else ["snd%d%d" % (t, i)])
        for i, (a, b) in enumerate(cfg["TCH"][t - 1] if t else cfg["XCH"]):
            tile = "p%d%d" % (t, i)
            mm("mp%d%d" % (t, i), tile, "qu2", "su2", 0, qt, st, a, b)
            cuts = [("eb%d%d" % (t, i), a, b, 1, spot("eb", a, b))]
            for r, (c, d) in enumerate(runs_):
                lo, hi = max(a, c), min(b, d)
                if lo < hi:
                    cuts.append(("ea%d%d%d" % (t, i, r), lo, hi, RADIX,
                                 ("eb", data(1, r) + (lo - c) // RADIX, data(1, r) + (hi - c) // RADIX)))
            for nm, lo, hi, step, o in cuts:
                num = ("it", H + lo, H + hi, step)
                add(nm, "ew", "V", [("#" + tile, 0, 1), num], [o],
                    lambda q, e, T, P, o=o, num=num, tile=tile, a=a: q.tensor_tensor(
                        ap(T, o), P(tile)[:, num[1] - H - a:num[2] - H - a:num[3]], ap(T, num), A.min), frees=tile)
        for i, (a, b) in enumerate(cfg["FCH"][t]):
            for p in range(4):
                tile = "f%d%d%d" % (t, i, p)
                mm("mf%d%d%d" % (t, i, p), tile, "qe", "se", 128 * p, qt, st, a, b)
                evac("fe%d%d%d" % (t, i, p), (ft, WW * p + H + a, WW * p + H + b), tile, b - a, 1.0 / 64)
        if not first:
            for p in range(4):
                tile = "h%d%d" % (t, p)
                mm("mh%d%d" % (t, p), tile, "qe", "se", 128 * p, "lq%d" % t, "ls%d" % t, 0, H)
                evac("he%d%d" % (t, p), (ft, WW * p, WW * p + H), tile, H, 1.0 / 64)
        for r in range(nr):
            for k in range(1, LEVELS + 1):
                level("e%d" % t, "eb", k, r, A.max, r in cfg["DUP"][t])
        tt("bl%d0" % t, ("rb", H, H + BLK), block("xb", 0), block("eb", 0), A.max)
        for n in range(1, NB):
            a, b = BLK * n, BLK * n + BLK
            gtt("bl%d%d" % (t, n), ("rb", H + a, H + b), ("rb", 0, H + a), ("lf", 4 * n, 4 * n + 4), block("eb", n), A.max)
        for n in range(NB):
            a, b = BLK * n, BLK * n + BLK
            hold("rs%d%d" % (t, n), ("rt%d" % t, a, b), ("rb", H + a, H + b), ("dd", 0, BLK))
        z, qz, sz, tn = "z%d" % t, "qz%d" % t, "sz%d" % t, "t%d" % (t + 1)
        for i, (a, b) in enumerate(cfg["ZB"][t]):
            g, lr = "%d%d" % (t, i), ("lr%d" % t, a // 16, b // 16)
            to_list("rl" + g, lr, ("rt%d" % t, a, b), 1.0)
            for p in range(4):
                gather("zg%s%d" % (g, p), (z, 4 * a + p, 4 * b, 4), (ft, WW * p, WW * p + H + b), lr)
        for i, (a, b) in enumerate(cfg["TCH"][t]):
            g = "%d%d" % (t, i)
            quant("qz" + g, qz, sz, a, b, z, 4 * a)
            for p in range(4):
                mm("me%s%d" % (g, p), "s%s%d" % (g, p), "qe", "se", 128 * p, qt, st, a, b, True, False,
                   after=["he%d%d" % (t, x) for x in range(4)])
            for p in range(4):
                mm("mw%s%d" % (g, p), "s%s%d" % (g, p), "wq", "wsc", 128 * p, qz, sz, a, b, False, True)
                evac("te%s%d" % (g, p), (tn, 4 * a + p, 4 * b, 4), "s%s%d" % (g, p), b - a, 1.0 / 64)
            quant("qt%d%d" % (t + 1, i), "qt%d" % (t + 1), "st%d" % (t + 1), a, b, tn, 4 * a)
    lin("ol", ("olb", 0, C), ("rb", H, WW), 1.0 / UNIT, float(C))
    store("sol", [("olb", 0, C)], lambda q, e, T, P: q.dma_start(T.ol[:, :], T.olb[0:128:16, :]))
    for i, (a, b) in enumerate(cfg["TCH"][ROUNDS - 1]):
        mm("my%d" % i, "y%d" % i, "qv", "sv", 0, "qt2", "st2", a, b)
        evac("ye%d" % i, ("yb", a, b), "y%d" % i, b - a, 1.0)
        store("sy%d" % i, [("yb", a, b)], lambda q, e, T, P, a=a, b=b: q.dma_start(T.y[:, a:b], T.yb[:, a:b]))
        store("sc%d" % i, [("qt2", a, b)],
              lambda q, e, T, P, a=a, b=b: q.dma_start(T.oc[:, 4 * a:4 * b], T.qt2[:, a:b].bitcast(dt.uint8)))
    for k in range(4):
        store("ss%d" % k, [("st2", 0, C)],
              lambda q, e, T, P, k=k: q.dma_start(T.osc[4 * k:4 * k + 4, :], T.st2[32 * k:32 * k + 4, :]))

    for j, o in enumerate(ops):
        o["deps"] = [p["name"] for p in ops[:j]
                     if any(_meet(a, b) for a in o["r"] + o["w"] for b in p["w"])
                     or (p["kind"] != "arrive" and any(_meet(a, b) for a in o["w"] for b in p["r"]))]
    return ops


def emit(g, core, T, topo, ops, order, prev, nxt):
    by = {o["name"]: o for o in ops}
    seq = [(n, e if e in by[n]["engs"] else by[n]["engs"][0]) for n, e in order if n in by]
    assert sorted(n for n, e in seq) == sorted(by)
    queue = {"V": g.vector, "S": g.scalar, "T": g.tensor, "G": g, "Y": g.sync}
    readers = {}
    for o in ops:
        if "frees" in o:
            readers.setdefault(o["frees"], []).append(o["name"])
    free, bank, waits, seen = [(b, []) for b in range(8)], {}, {}, set()
    for n, e in seq:
        o = by[n]
        d = [] if o["kind"] == "arrive" else list(o["deps"])
        if o.get("start"):
            bank[o["tile"]], who = free.pop(0)
            d += who
        elif o["kind"] == "mm":
            d = [x for x in d if by[x].get("tile") != o["tile"]]
        seen.add(n)
        if "frees" in o and seen.issuperset(readers[o["frees"]]):
            free.append((bank[o["frees"]], readers[o["frees"]]))
        waits[n] = d
    needed = set(x for d in waits.values() for x in d)
    total, done, known = {}, {}, {e: {} for e in queue}

    def bump(s, k):
        total[s] = total.get(s, 0) + k
        return s, total[s]

    for n, e in seq:
        o = by[n]
        LABEL[0] = n
        if o["kind"] == "arrive":
            done[n] = (bump(n, 2 * len(topo.engines(prev, core))), {})
            continue
        q, kn = queue[e], known[e]
        want = {}
        for x in waits[n]:
            (s, k), clock = done[x]
            if want.get(s, (0, None))[0] < k:
                want[s] = (k, clock)
        for s, (k, clock) in want.items():
            if kn.get(s, 0) < k and not any(c.get(s, 0) >= k for s2, (k2, c) in want.items() if s2 != s):
                q.wait_ge(T.sem[s], k)
        for s, (k, clock) in want.items():
            for s2, k2 in list(clock.items()) + [(s, k)]:
                kn[s2] = max(kn.get(s2, 0), k2)
        if o["kind"] == "send":
            rid, pid, _ = topo.addr(nxt)
            t, m = o["t"], topo.mask(core, nxt)
            a, b = o["cut"]
            g.remote_dma(T["lq%d" % t][:, a - C + H:b - C + H].bitcast(dt.uint8), T["qt%d" % t][:, a:b].bitcast(dt.uint8),
                         T.sem[o["sem"]], T.sem.sent, pid, rid, m)
            g.remote_dma(T["ls%d" % t][:, a - C + H:b - C + H], T["st%d" % t][:, a:b], T.sem[o["sem"]], T.sem.sent, pid, rid, m)
            bump("sent", 2 * len(topo.engines(core, nxt)))
            continue
        ins = o["em"](q, e, T, lambda tile: T["ps%d" % bank[tile]])
        if o["kind"] == "load":
            ins.then_inc(T.sem[n], 16)
            done[n] = (bump(n, 16), dict(kn))
        elif o["kind"] == "store":
            ins.then_inc(T.sem["out" + e], 16)
            bump("out" + e, 16)
        elif n in needed:
            ins.then_inc(T.sem["c" + e], 1)
            done[n] = (bump("c" + e, 1), dict(kn))
    for s in ("sent", "outY", "outS"):
        if s in total:
            g.wait_ge(T.sem[s], total[s])


def rank_program(g, core, T, topo):
    rank = T.rank_of(core)
    if rank is None:
        return
    prev = T.cores[rank - 1] if rank > 0 else None
    nxt = T.cores[rank + 1] if rank + 1 < len(T.cores) else None
    assert nxt is None or topo.may_write(core, nxt)
    emit(g, core, T, topo, plan(prev is None, nxt is None, CFG), [(w[:-1], w[-1]) for w in ORDER.split()], prev, nxt)
